import numpy as np
import ml_dtypes


def mxq(x, axis, fmt="e4m3"):
    dtype, down = {"e4m3": (ml_dtypes.float8_e4m3fn, 7), "e5m2": (ml_dtypes.float8_e5m2, 14)}[fmt]
    v = np.moveaxis(np.asarray(x, np.float32).astype(ml_dtypes.bfloat16).astype(np.float64), axis, -1)
    blocks = v.reshape(v.shape[:-1] + (-1, 32))
    amax = np.abs(blocks).max(-1, keepdims=True)
    byte = np.maximum(np.where(amax > 0, np.frexp(amax)[1] - 1 + 127, 0) - down, 1)
    scale = np.exp2(byte - 127.0)
    codes = (blocks / scale).astype(np.float32).astype(dtype).astype(np.float64)
    return np.moveaxis((codes * scale).reshape(v.shape), -1, axis)


WIDE = False


def mx_kscale(k):
    if not WIDE:
        return np.ones(k)
    levels = np.array([10, -10, 5, -5, 0])
    if k % 512:
        return np.exp2(np.random.permutation(np.resize(levels, k // 32))).repeat(32)
    a = np.empty((k // 512, 16))
    for p in range(k // 512):
        a[p, :8] = np.random.permutation(np.resize(levels, 8))
        for g in range(8):
            far = levels[np.abs(levels - a[p, g]) >= 10]
            a[p, g + 8] = far[np.random.randint(len(far))]
    return np.exp2(a.ravel()).repeat(32)


def f64(x):
    return np.asarray(x).astype(np.float64)


def striped(idx):
    return np.tile(idx.reshape(-1, 16).T, (8, 1)).astype(np.uint16)


def unstriped(offs):
    return offs[:16].T.reshape(-1).astype(np.int64)


E2M1 = np.array([0.0, 0.5, 1.0, 1.5, 2.0, 3.0, 4.0, 6.0, -0.0, -0.5, -1.0, -1.5, -2.0, -3.0, -4.0, -6.0])


def pack_weight(w, fmt):
    k, n = w.shape
    w = f64(np.asarray(w, np.float32).astype(ml_dtypes.bfloat16)).reshape(k // 32, 32, n)
    amax = np.abs(w).max(1)
    if fmt == "e4m3":
        byte = np.frexp(amax)[1] - 1 + 127 - 7
    else:
        mant, ex = np.frexp(amax / 6.0)
        byte = np.where(mant > 0.5, ex, ex - 1) + 127
    byte = np.clip(np.where(amax > 0, byte, 1), 1, 254)
    scaled = (w * np.exp2(127.0 - byte)[:, None, :]).reshape(k, n).astype(np.float32)
    by_word = np.ascontiguousarray(scaled.reshape(k // 512, 128, 4, n).transpose(0, 1, 3, 2))
    if fmt == "e4m3":
        words = by_word.astype(ml_dtypes.float8_e4m3fn).view(np.uint8)
    else:
        c = by_word.astype(ml_dtypes.float4_e2m1fn).view(np.uint8) & 0xF
        words = (c[..., 0::2] | (c[..., 1::2] << 4)).reshape(k // 512, 128, 2 * n)
    return np.ascontiguousarray(words), np.ascontiguousarray(byte.astype(np.uint8).reshape(k // 512, 16, n))


def unpack_weight(words, scales, fmt):
    g, _, n = scales.shape
    words = np.ascontiguousarray(words).reshape(g, 128, n, -1)
    if fmt == "e4m3":
        vals = words.view(ml_dtypes.float8_e4m3fn).astype(np.float64)
    else:
        nib = np.empty((g, 128, n, 4), np.uint8)
        nib[..., 0::2] = words & 0xF
        nib[..., 1::2] = words >> 4
        vals = E2M1[nib]
    vals = vals * np.repeat(np.exp2(scales.astype(np.float64) - 127.0), 8, axis=1)[..., None]
    return vals.transpose(0, 1, 3, 2).reshape(g * 512, n)


def gelu(v):
    return 0.5 * v * (1.0 + np.tanh(np.sqrt(2.0 / np.pi) * (v + 0.044715 * v**3)))


K, T, E, C, H, N = 2560, 512, 4, 256, 512, 256


def by_expert(wq, xq):
    return np.concatenate([wq[e].T @ xq[:, e * C:(e + 1) * C] for e in range(E)], axis=1)


def setup_inputs():
    n = np.random.standard_normal
    s = mx_kscale(K)[:, None]
    u = mx_kscale(H)
    first = np.random.permutation(np.repeat(np.arange(E), T // E))
    second = (first + 1 + np.random.permutation(np.repeat(np.arange(E - 1), -(-T // (E - 1)))[:T])) % E
    while np.bincount(second, minlength=E).max() != T // E:
        load = np.bincount(second, minlength=E); hi, lo = int(load.argmax()), int(load.argmin())
        t = np.flatnonzero((second == hi) & (first != lo))[0]; second[t] = lo
    slot_token = np.empty(E * C, np.int64); pos = np.empty((2, T), np.int64); fill = np.zeros(E, np.int64)
    place = np.stack([np.random.permutation(C) for _ in range(E)])
    for r, deal in enumerate((first, second)):
        for t in np.random.permutation(T):
            e = deal[t]; j = e * C + place[e, fill[e]]; fill[e] += 1; slot_token[j] = t; pos[r, t] = j
    g = np.random.uniform(0.2, 0.8, T)
    x = pack_weight(n((K, T)) * s, "e4m3")
    return {
        "x_words": x[0],
        "x_scales": x[1],
        "w1": (n((E, K, H)) / np.sqrt(K) / s[None] * u[None, None, :]).astype(np.float32),
        "w2": (n((E, H, N)) / np.sqrt(H) / u[None, :, None]).astype(np.float32),
        "gate": np.stack([np.tile(g, (N, 1)), np.tile(1.0 - g, (N, 1))]).astype(np.float32),
        "offs": striped(slot_token),
        "pos1": striped(pos[0]),
        "pos2": striped(pos[1]),
    }


def reference(x_words, x_scales, w1, w2, gate, offs, pos1, pos2):
    idx = unstriped(offs)
    xq = unpack_weight(x_words, x_scales, "e4m3")[:, idx]
    h = gelu(by_expert(mxq(f64(w1), 1, "e4m3"), xq))
    y = by_expert(mxq(f64(w2), 1, "e4m3"), mxq(h, 0, "e4m3"))
    return f64(gate[0]) * y[:, unstriped(pos1)] + f64(gate[1]) * y[:, unstriped(pos2)]

@@ -1,0 +1,250 @@
+from contextlib import ExitStack
+
+import concourse.mybir as mybir
+
+K, T, E, C, H, N = 2560, 512, 4, 256, 512, 256
+FLOPS = 2 * E * C * (K * H + H * N)
+
+F32 = mybir.dt.float32
+BF16 = mybir.dt.bfloat16
+I32 = mybir.dt.int32
+U32 = mybir.dt.uint32
+U16 = mybir.dt.uint16
+U8 = mybir.dt.uint8
+FP8X4 = mybir.dt.float8_e4m3fn_x4
+GELU = mybir.ActivationFunctionType.Gelu_apprx_tanh
+MULT = mybir.AluOpType.mult
+ADD = mybir.AluOpType.add
+
+P = 128
+PACK = 4
+K_PASS = P * PACK
+PASSES = K // K_PASS
+PLANES = 4
+SLOTS = E * C
+HALF = 128
+N_TILES = N // P
+LIST_COLS = 16
+RAW_BUFS = 9
+VECTOR_CHUNKS = (5, 9, 12, 14, 16, 18)
+PAIR = 2 * C
+WINDOW = 768
+SCALAR_M_LAST = 44
+
+
+def tile_moe_pkd_mlp_gelu_kernel(tc, x_words, x_scales, w1, w2, gate, offs, pos1, pos2, out):
+    nc = tc.nc
+    with ExitStack() as ctx:
+        keep = ctx.enter_context(tc.tile_pool(name="keep", bufs=1))
+        raws = ctx.enter_context(tc.tile_pool(name="raws", bufs=RAW_BUFS))
+        stage = ctx.enter_context(tc.tile_pool(name="stage", bufs=4))
+        codes = ctx.enter_context(tc.tile_pool(name="codes", bufs=2 * PASSES))
+        acc = ctx.enter_context(tc.psum_pool(name="acc", bufs=6))
+        yacc = ctx.enter_context(tc.psum_pool(name="yacc", bufs=2))
+
+        offs_sb = keep.tile([P, SLOTS // LIST_COLS], U16, name="offs_sb")
+        pos_sb = [keep.tile([P, T // LIST_COLS], U16, name="pos_sb%d" % r) for r in range(2)]
+        tok_words = keep.tile([P, (PASSES - 1) * T + WINDOW], I32, name="tok_words", align_bytes=64)
+        tok_scales = keep.tile([P, T + WINDOW], U8, name="tok_scales", align_bytes=64)
+        slot_words = [keep.tile([P, PASSES, PAIR], U32, name="slot_words%d" % g, align_bytes=64) for g in range(2)]
+        slot_scales = [keep.tile([P, 2, PAIR], U8, name="slot_scales%d" % g, align_bytes=64) for g in range(2)]
+        h_codes = [keep.tile([P, C], U32, name="h_codes%d" % e, align_bytes=64) for e in range(E)]
+        h_scales = [keep.tile([P, C], U8, name="h_scales%d" % e, align_bytes=64) for e in range(E)]
+        y_sb = [keep.tile([P, SLOTS], F32, name="y_sb%d" % nt) for nt in range(N_TILES)]
+
+        nc.vector.memset(tok_scales[:].bitcast(I32), 0)
+        nc.vector.memset(tok_words[:, PASSES * T :], 0)
+
+        def load_scale_rows(d):
+            q = d % 4
+            if d < 4:
+                nc.sync.dma_start(
+                    out=tok_scales[32 * q : 32 * q + 16, 0:T].bitcast(I32),
+                    in_=x_scales[0:PLANES, 4 * q : 4 * q + 4, :].bitcast(I32),
+                )
+            else:
+                nc.sync.dma_start(
+                    out=tok_scales[32 * q : 32 * q + 4, T : 2 * T].bitcast(I32),
+                    in_=x_scales[PLANES, 4 * q : 4 * q + 4, :].bitcast(I32),
+                )
+
+        def load_w1(e, o):
+            raw = raws.tile([P, PACK, H], F32, name="raw")
+            nc.sync.dma_start(out=raw[:], in_=w1[e, o * K_PASS : (o + 1) * K_PASS, :].rearrange("(p j) i -> p j i", j=PACK))
+            return raw
+
+        def load_w2(e):
+            raw = raws.tile([P, PACK, N], F32, name="raw")
+            nc.sync.dma_start(out=raw[:], in_=w2[e].rearrange("(p j) n -> p j n", j=PACK))
+            return raw
+
+        def load_gate(nt):
+            raw = raws.tile([P, 2, T], F32, name="raw")
+            nc.sync.dma_start(out=raw[:], in_=gate[:, nt * P : (nt + 1) * P, :].rearrange("r p t -> p r t"))
+            return raw
+
+        def cast_w1(raw, split):
+            grouped = stage.tile([P, PACK, P, PACK], BF16, name="w1_grouped", align_bytes=64, bufs=8)
+            src = raw[:].rearrange("p j (m t) -> p m j t", t=PACK)
+            dst = grouped[:].rearrange("p t m j -> p m j t")
+            if split > 0:
+                nc.scalar.copy(out=dst[:, 0:split], in_=src[:, 0:split])
+            if split < P:
+                nc.vector.tensor_copy(out=dst[:, split:P], in_=src[:, split:P])
+            return grouped
+
+        def quantize_w1(grouped):
+            wc = codes.tile([P, H], U32, name="w1_codes", align_bytes=64)
+            ws = codes.tile([P, H], U8, name="w1_scales", align_bytes=64)
+            nc.vector.quantize_mx(out=wc[:].bitcast(FP8X4), scales=ws[:], in_=grouped[:].rearrange("p t m j -> p (t m j)"))
+            return wc, ws
+
+        def gather_words(g, o):
+            lst = offs_sb[:, g * (PAIR // LIST_COLS) : (g + 1) * (PAIR // LIST_COLS)]
+            window = tok_words[:, o * T : o * T + WINDOW].bitcast(U32)
+            nc.vector.tensor_copy(out=slot_words[g][:, o, :], in_=window.indirect(lst))
+
+        def gather_scales(g, b):
+            lst = offs_sb[:, g * (PAIR // LIST_COLS) : (g + 1) * (PAIR // LIST_COLS)]
+            nc.vector.tensor_copy(out=slot_scales[g][:, b, :], in_=tok_scales[:, b * T : b * T + WINDOW].indirect(lst))
+
+        def layer1_pass(dst, e, o, t, wq, cols):
+            wc, ws = wq
+            first_row = 4 * (o % PLANES)
+            g = e // 2
+            slots = slice((e % 2) * C + cols.start, (e % 2) * C + cols.stop)
+            nc.tensor.matmul_mx(
+                out=dst,
+                lhsT=wc[:, t * P : (t + 1) * P].bitcast(FP8X4),
+                lhsT_scale=ws[:, t * P : (t + 1) * P],
+                rhs=slot_words[g][:, o, slots].bitcast(FP8X4),
+                rhs_scale=slot_scales[g][first_row:P, o // PLANES, slots],
+                start=(o == 0),
+                stop=(o == PASSES - 1),
+            )
+
+        def quantize_h(e, grouped):
+            nc.vector.quantize_mx(
+                out=h_codes[e][:].bitcast(FP8X4), scales=h_scales[e][:], in_=grouped[:].rearrange("p c t -> p (c t)")
+            )
+
+        def gelu_planes(banks):
+            planes = stage.tile([P, PACK, C], BF16, name="h_planes", bufs=2)
+            for t in range(PACK):
+                nc.scalar.activation(out=planes[:, t, :], in_=banks[t][:], func=GELU)
+            return planes
+
+        def interleave_h(planes):
+            grouped = stage.tile([P, C, PACK], BF16, name="h_grouped", align_bytes=64, bufs=2)
+            nc.vector.tensor_copy(out=grouped[:], in_=planes[:].rearrange("p t c -> p c t"))
+            return grouped
+
+        def load_words(o):
+            nc.sync.dma_start(out=tok_words[:, o * T : (o + 1) * T], in_=x_words[o].rearrange("p t r -> p (t r)").bitcast(I32))
+
+        def layer2(e, raw, on_scalar):
+            grouped = stage.tile([P, N, PACK], BF16, name="w2_grouped", align_bytes=64)
+            src = raw[:].rearrange("p j (c u) -> p c j u", u=4)
+            dst = grouped[:].rearrange("p (c u) j -> p c j u", u=4)
+            if on_scalar:
+                nc.scalar.copy(out=dst, in_=src)
+            else:
+                nc.vector.tensor_copy(out=dst, in_=src)
+            wc = stage.tile([P, N], U32, name="w2_codes", align_bytes=64)
+            ws = stage.tile([P, N], U8, name="w2_scales", align_bytes=64)
+            nc.vector.quantize_mx(out=wc[:].bitcast(FP8X4), scales=ws[:], in_=grouped[:].rearrange("p n j -> p (n j)"))
+            return wc, ws
+
+        def layer2_product(e, wq):
+            wc, ws = wq
+            bank = yacc.tile([P, N_TILES, C], F32, name="yacc")
+            for nt in range(N_TILES):
+                nc.tensor.matmul_mx(
+                    out=bank[:, nt, :],
+                    lhsT=wc[:, nt * P : (nt + 1) * P].bitcast(FP8X4),
+                    lhsT_scale=ws[:, nt * P : (nt + 1) * P],
+                    rhs=h_codes[e][:].bitcast(FP8X4),
+                    rhs_scale=h_scales[e][:],
+                    start=True,
+                    stop=True,
+                )
+            for nt in range(N_TILES):
+                nc.scalar.copy(out=y_sb[nt][:, e * C : (e + 1) * C], in_=bank[:, nt, :])
+
+        nc.sync.dma_start(offs_sb[:], offs)
+        load_words(0)
+        load_words(1)
+        last = E - 1
+        planes = None
+        w2_first = None
+        wqs = []
+        banks = []
+        h_grouped = None
+        pending = [(0, 0), (0, 1)] + [(o, 0) for o in range(1, PASSES + 2)] + [(o, 1) for o in range(1, PASSES + 2)]
+
+        def gather_next(count):
+            for g in range(min(count, len(pending))):
+                kind, e = pending[0]
+                pending.remove(pending[0])
+                if kind < PASSES:
+                    gather_words(e, kind)
+                else:
+                    gather_scales(e, kind - PASSES)
+
+        gather_next(2)
+        for e in range(E):
+            wqs = []
+            for o in range(PASSES):
+                raw = load_w1(e, o)
+                if e == 0 and o == 0:
+                    for oo in range(2, PASSES):
+                        load_words(oo)
+                        load_scale_rows(oo - 2)
+                    load_scale_rows(3)
+                if e == 0 and o in (1, 2):
+                    load_scale_rows(2 * o + 2)
+                    load_scale_rows(2 * o + 3)
+                if e == 0 and o == 3:
+                    nc.sync.dma_start(pos_sb[0][:], pos1)
+                    nc.sync.dma_start(pos_sb[1][:], pos2)
+                if e == last and o == 0:
+                    w2_first = load_w2(0)
+                is_end = e == last and o == PASSES - 1
+                n = e * PASSES + o
+                grouped = cast_w1(raw, SCALAR_M_LAST if is_end else (0 if n in VECTOR_CHUNKS else P))
+                gather_next(2 if n == 0 else 1)
+                wqs.append(quantize_w1(grouped))
+                if e > 0 and o == 0:
+                    planes = gelu_planes(banks)
+                if e > 0 and o == 1:
+                    h_grouped = interleave_h(planes)
+                if e > 0 and o == 2:
+                    quantize_h(e - 1, h_grouped)
+                if e == last and o == 2:
+                    layer2_product(0, layer2(0, w2_first, True))
+                first = PASSES - 1 if e == 0 else 0
+                if o == first:
+                    banks = [acc.tile([P, C], F32, name="acc") for t in range(PACK)]
+                if o >= first:
+                    for oo in (range(o + 1) if o == first else [o]):
+                        for t in range(PACK):
+                            layer1_pass(banks[t][:], e, oo, t, wqs[oo], slice(0, C))
+
+        w2_raw = [load_w2(e) for e in range(1, E)]
+        gates = [load_gate(nt) for nt in range(N_TILES)]
+
+        quantize_h(last, interleave_h(gelu_planes(banks)))
+        for e in range(1, E):
+            layer2_product(e, layer2(e, w2_raw[e - 1], e == 1))
+
+        for nt in range(N_TILES):
+            width = T if nt == 0 else T // 2
+            for t0 in range(0, T, width):
+                cols = slice(t0, t0 + width)
+                lst = slice(t0 // LIST_COLS, (t0 + width) // LIST_COLS)
+                prods = [stage.tile([P, width], F32, name="prod") for r in range(2)]
+                for r in range(2):
+                    nc.vector.tensor_tensor(prods[r][:], y_sb[nt][:].indirect(pos_sb[r][:, lst]), gates[nt][:, r, cols], MULT)
+                res = stage.tile([P, width], F32, name="res")
+                nc.vector.tensor_tensor(res[:], prods[0][:], prods[1][:], ADD)
+                nc.sync.dma_start(out=out[nt * P : (nt + 1) * P, cols], in_=res[:])

@@ -25,48 +25,58 @@ SLOTS = E * C
 HALF = 128
 N_TILES = N // P
 LIST_COLS = 16
-RAW_BUFS = 9
-VECTOR_CHUNKS = (5, 9, 12, 14, 16, 18)
 PAIR = 2 * C
 WINDOW = 768
-SCALAR_M_LAST = 44
+CHUNKS = E * PASSES
+SCALAR_SHARE = [128,128,128,128,0,128,128,0,128,128,0,128,0,128,0,128,0,80,44,44]
+W2_SHARE = [64,64,0,32]
+EARLY_W2 = {13:0}
+W2_TURN = {3:"after_matmul"}
+GATHERS = [1,1,1,1,1,1,1,1,1,1,1,1,1,1,1,1,1,1,1,1]
 
 
 def tile_moe_pkd_mlp_gelu_kernel(tc, x_words, x_scales, w1, w2, gate, offs, pos1, pos2, out):
     nc = tc.nc
     with ExitStack() as ctx:
         keep = ctx.enter_context(tc.tile_pool(name="keep", bufs=1))
-        raws = ctx.enter_context(tc.tile_pool(name="raws", bufs=RAW_BUFS))
+        raws = ctx.enter_context(tc.tile_pool(name="raws", bufs=9))
         stage = ctx.enter_context(tc.tile_pool(name="stage", bufs=4))
-        codes = ctx.enter_context(tc.tile_pool(name="codes", bufs=2 * PASSES))
-        acc = ctx.enter_context(tc.psum_pool(name="acc", bufs=6))
-        yacc = ctx.enter_context(tc.psum_pool(name="yacc", bufs=2))
+        codes = ctx.enter_context(tc.tile_pool(name="codes", bufs=10))
+        turn = ctx.enter_context(tc.tile_pool(name="turn", bufs=1))
+        acc = ctx.enter_context(tc.psum_pool(name="acc", bufs=4))
+        yacc = ctx.enter_context(tc.psum_pool(name="yacc", bufs=4))
 
         offs_sb = keep.tile([P, SLOTS // LIST_COLS], U16, name="offs_sb")
         pos_sb = [keep.tile([P, T // LIST_COLS], U16, name="pos_sb%d" % r) for r in range(2)]
         tok_words = keep.tile([P, (PASSES - 1) * T + WINDOW], I32, name="tok_words", align_bytes=64)
-        tok_scales = keep.tile([P, T + WINDOW], U8, name="tok_scales", align_bytes=64)
+        tok_scales = keep.tile([P, 2, WINDOW], U8, name="tok_scales", align_bytes=64)
         slot_words = [keep.tile([P, PASSES, PAIR], U32, name="slot_words%d" % g, align_bytes=64) for g in range(2)]
         slot_scales = [keep.tile([P, 2, PAIR], U8, name="slot_scales%d" % g, align_bytes=64) for g in range(2)]
         h_codes = [keep.tile([P, C], U32, name="h_codes%d" % e, align_bytes=64) for e in range(E)]
         h_scales = [keep.tile([P, C], U8, name="h_scales%d" % e, align_bytes=64) for e in range(E)]
         y_sb = [keep.tile([P, SLOTS], F32, name="y_sb%d" % nt) for nt in range(N_TILES)]
 
-        nc.vector.memset(tok_scales[:].bitcast(I32), 0)
+        nc.vector.memset(tok_scales[:].rearrange("p b t -> p (b t)").bitcast(I32), 0)
         nc.vector.memset(tok_words[:, PASSES * T :], 0)
 
         def load_scale_rows(d):
             q = d % 4
             if d < 4:
                 nc.sync.dma_start(
-                    out=tok_scales[32 * q : 32 * q + 16, 0:T].bitcast(I32),
+                    out=tok_scales[32 * q : 32 * q + 16, 0, 0:T].bitcast(I32),
                     in_=x_scales[0:PLANES, 4 * q : 4 * q + 4, :].bitcast(I32),
                 )
             else:
                 nc.sync.dma_start(
-                    out=tok_scales[32 * q : 32 * q + 4, T : 2 * T].bitcast(I32),
+                    out=tok_scales[32 * q : 32 * q + 4, 1, 0:T].bitcast(I32),
                     in_=x_scales[PLANES, 4 * q : 4 * q + 4, :].bitcast(I32),
                 )
+
+        def load_words(o0, o1):
+            nc.sync.dma_start(
+                out=tok_words[:, o0 * T : o1 * T].rearrange("p (o t) -> p o t", t=T),
+                in_=x_words[o0:o1].rearrange("o p t r -> p o (t r)").bitcast(I32),
+            )
 
         def load_w1(e, o):
             raw = raws.tile([P, PACK, H], F32, name="raw")
@@ -83,52 +93,64 @@ def tile_moe_pkd_mlp_gelu_kernel(tc, x_words, x_scales, w1, w2, gate, offs, pos1
             nc.sync.dma_start(out=raw[:], in_=gate[:, nt * P : (nt + 1) * P, :].rearrange("r p t -> p r t"))
             return raw
 
-        def cast_w1(raw, split):
-            grouped = stage.tile([P, PACK, P, PACK], BF16, name="w1_grouped", align_bytes=64, bufs=8)
-            src = raw[:].rearrange("p j (m t) -> p m j t", t=PACK)
-            dst = grouped[:].rearrange("p t m j -> p m j t")
+        def shared_cast(dst, src, split):
+            total = dst.shape[1]
             if split > 0:
                 nc.scalar.copy(out=dst[:, 0:split], in_=src[:, 0:split])
-            if split < P:
-                nc.vector.tensor_copy(out=dst[:, split:P], in_=src[:, split:P])
+            if split < total:
+                nc.vector.tensor_copy(out=dst[:, split:total], in_=src[:, split:total])
+
+        def cast_w1(raw, split):
+            grouped = stage.tile([P, PACK, P, PACK], BF16, name="w1_grouped", align_bytes=64, bufs=8)
+            shared_cast(grouped[:].rearrange("p t m j -> p m j t"), raw[:].rearrange("p j (m t) -> p m j t", t=PACK), split)
             return grouped
 
-        def quantize_w1(grouped):
-            wc = codes.tile([P, H], U32, name="w1_codes", align_bytes=64)
+        def quantize_w1(grouped, pieces):
+            pool, tag = (turn, "after_matmul") if pieces > 1 else (codes, "w1_codes")
+            wc = pool.tile([P, H], U32, name="w1_codes", tag=tag, align_bytes=64)
             ws = codes.tile([P, H], U8, name="w1_scales", align_bytes=64)
-            nc.vector.quantize_mx(out=wc[:].bitcast(FP8X4), scales=ws[:], in_=grouped[:].rearrange("p t m j -> p (t m j)"))
+            flat = grouped[:].rearrange("p t m j -> p (t m j)")
+            width = H // pieces
+            for c0 in range(0, H, width):
+                nc.vector.quantize_mx(
+                    out=wc[:, c0 : c0 + width].bitcast(FP8X4),
+                    scales=ws[:, c0 : c0 + width],
+                    in_=flat[:, PACK * c0 : PACK * (c0 + width)],
+                )
             return wc, ws
 
-        def gather_words(g, o):
+        def gather(kind, g):
             lst = offs_sb[:, g * (PAIR // LIST_COLS) : (g + 1) * (PAIR // LIST_COLS)]
-            window = tok_words[:, o * T : o * T + WINDOW].bitcast(U32)
-            nc.vector.tensor_copy(out=slot_words[g][:, o, :], in_=window.indirect(lst))
+            if kind < PASSES:
+                window = tok_words[:, kind * T : kind * T + WINDOW].bitcast(U32)
+                nc.vector.tensor_copy(out=slot_words[g][:, kind, :], in_=window.indirect(lst))
+            else:
+                b = kind - PASSES
+                nc.vector.tensor_copy(out=slot_scales[g][:, b, :], in_=tok_scales[:, b, :].indirect(lst))
 
-        def gather_scales(g, b):
-            lst = offs_sb[:, g * (PAIR // LIST_COLS) : (g + 1) * (PAIR // LIST_COLS)]
-            nc.vector.tensor_copy(out=slot_scales[g][:, b, :], in_=tok_scales[:, b * T : b * T + WINDOW].indirect(lst))
-
-        def layer1_pass(dst, e, o, t, wq, cols):
+        def layer1_pass(dst, e, o, t, wq, c0, c1, start, stop):
             wc, ws = wq
             first_row = 4 * (o % PLANES)
             g = e // 2
-            slots = slice((e % 2) * C + cols.start, (e % 2) * C + cols.stop)
+            slots = slice((e % 2) * C + c0, (e % 2) * C + c1)
             nc.tensor.matmul_mx(
                 out=dst,
                 lhsT=wc[:, t * P : (t + 1) * P].bitcast(FP8X4),
                 lhsT_scale=ws[:, t * P : (t + 1) * P],
                 rhs=slot_words[g][:, o, slots].bitcast(FP8X4),
                 rhs_scale=slot_scales[g][first_row:P, o // PLANES, slots],
-                start=(o == 0),
-                stop=(o == PASSES - 1),
+                start=start,
+                stop=stop,
             )
 
-        def quantize_h(e, grouped):
-            nc.vector.quantize_mx(
-                out=h_codes[e][:].bitcast(FP8X4), scales=h_scales[e][:], in_=grouped[:].rearrange("p c t -> p (c t)")
-            )
+        def open_banks():
+            return [acc.tile([P, C], F32, name="acc") for t in range(PACK)]
 
-        def gelu_planes(banks):
+        def layer1_step(banks, e, o, wq):
+            for t in range(PACK):
+                layer1_pass(banks[t][:], e, o, t, wq, 0, C, o == 0, o == PASSES - 1)
+
+        def gelu(banks):
             planes = stage.tile([P, PACK, C], BF16, name="h_planes", bufs=2)
             for t in range(PACK):
                 nc.scalar.activation(out=planes[:, t, :], in_=banks[t][:], func=GELU)
@@ -136,20 +158,25 @@ def tile_moe_pkd_mlp_gelu_kernel(tc, x_words, x_scales, w1, w2, gate, offs, pos1
 
         def interleave_h(planes):
             grouped = stage.tile([P, C, PACK], BF16, name="h_grouped", align_bytes=64, bufs=2)
-            nc.vector.tensor_copy(out=grouped[:], in_=planes[:].rearrange("p t c -> p c t"))
+            nc.vector.tensor_copy(
+                out=grouped[:].rearrange("p (c u) t -> p c t u", u=4), in_=planes[:].rearrange("p t (c u) -> p c t u", u=4)
+            )
             return grouped
 
-        def load_words(o):
-            nc.sync.dma_start(out=tok_words[:, o * T : (o + 1) * T], in_=x_words[o].rearrange("p t r -> p (t r)").bitcast(I32))
+        def quantize_h(e, grouped):
+            nc.vector.quantize_mx(
+                out=h_codes[e][:].bitcast(FP8X4), scales=h_scales[e][:], in_=grouped[:].rearrange("p c t -> p (c t)")
+            )
 
-        def layer2(e, raw, on_scalar):
-            grouped = stage.tile([P, N, PACK], BF16, name="w2_grouped", align_bytes=64)
-            src = raw[:].rearrange("p j (c u) -> p c j u", u=4)
-            dst = grouped[:].rearrange("p (c u) j -> p c j u", u=4)
-            if on_scalar:
-                nc.scalar.copy(out=dst, in_=src)
-            else:
-                nc.vector.tensor_copy(out=dst, in_=src)
+        def cast_w2(e, raw):
+            pool, tag = (turn, W2_TURN[e]) if e in W2_TURN else (stage, "w2_grouped")
+            grouped = pool.tile([P, N, PACK], BF16, name="w2_grouped", tag=tag, align_bytes=64)
+            shared_cast(
+                grouped[:].rearrange("p (c u) j -> p c j u", u=4), raw[:].rearrange("p j (c u) -> p c j u", u=4), W2_SHARE[e]
+            )
+            return grouped
+
+        def quantize_w2(grouped):
             wc = stage.tile([P, N], U32, name="w2_codes", align_bytes=64)
             ws = stage.tile([P, N], U8, name="w2_scales", align_bytes=64)
             nc.vector.quantize_mx(out=wc[:].bitcast(FP8X4), scales=ws[:], in_=grouped[:].rearrange("p n j -> p (n j)"))
@@ -157,10 +184,14 @@ def tile_moe_pkd_mlp_gelu_kernel(tc, x_words, x_scales, w1, w2, gate, offs, pos1
 
         def layer2_product(e, wq):
             wc, ws = wq
-            bank = yacc.tile([P, N_TILES, C], F32, name="yacc")
+            if e == E - 1:
+                bank = [yacc.tile([P, C], F32, name="yacc")[:] for nt in range(N_TILES)]
+            else:
+                both = yacc.tile([P, N_TILES, C], F32, name="yacc")
+                bank = [both[:, nt, :] for nt in range(N_TILES)]
             for nt in range(N_TILES):
                 nc.tensor.matmul_mx(
-                    out=bank[:, nt, :],
+                    out=bank[nt],
                     lhsT=wc[:, nt * P : (nt + 1) * P].bitcast(FP8X4),
                     lhsT_scale=ws[:, nt * P : (nt + 1) * P],
                     rhs=h_codes[e][:].bitcast(FP8X4),
@@ -168,83 +199,97 @@ def tile_moe_pkd_mlp_gelu_kernel(tc, x_words, x_scales, w1, w2, gate, offs, pos1
                     start=True,
                     stop=True,
                 )
-            for nt in range(N_TILES):
-                nc.scalar.copy(out=y_sb[nt][:, e * C : (e + 1) * C], in_=bank[:, nt, :])
+            return bank
 
+        def copy_y(e, bank, nt):
+            nc.scalar.copy(out=y_sb[nt][:, e * C : (e + 1) * C], in_=bank[nt])
+
+        load_words(0, 2)
         nc.sync.dma_start(offs_sb[:], offs)
-        load_words(0)
-        load_words(1)
+        for d in range(4):
+            load_scale_rows(d)
         last = E - 1
-        planes = None
-        w2_first = None
-        wqs = []
-        banks = []
-        h_grouped = None
-        pending = [(0, 0), (0, 1)] + [(o, 0) for o in range(1, PASSES + 2)] + [(o, 1) for o in range(1, PASSES + 2)]
+        pending = [(0, 0), (5, 0), (0, 1), (1, 0), (2, 0), (3, 0), (4, 0), (6, 0), (5, 1), (1, 1), (2, 1), (3, 1), (4, 1), (6, 1)]
+        later = {}
 
         def gather_next(count):
-            for g in range(min(count, len(pending))):
-                kind, e = pending[0]
-                pending.remove(pending[0])
-                if kind < PASSES:
-                    gather_words(e, kind)
-                else:
-                    gather_scales(e, kind - PASSES)
+            for kind, g in pending[0:count]:
+                gather(kind, g)
+                pending.remove((kind, g))
 
-        gather_next(2)
+        gather_next(3)
+        banks = []
+        h_stage = None
         for e in range(E):
             wqs = []
             for o in range(PASSES):
+                n = e * PASSES + o
+                if n in EARLY_W2:
+                    later[n] = load_w2(EARLY_W2[n])
                 raw = load_w1(e, o)
-                if e == 0 and o == 0:
-                    for oo in range(2, PASSES):
-                        load_words(oo)
-                        load_scale_rows(oo - 2)
-                    load_scale_rows(3)
-                if e == 0 and o in (1, 2):
-                    load_scale_rows(2 * o + 2)
-                    load_scale_rows(2 * o + 3)
-                if e == 0 and o == 3:
+                if n == 0:
+                    load_words(2, PASSES)
+                if n == 0:
+                    for d in range(4, 8):
+                        load_scale_rows(d)
+                if n == 5:
                     nc.sync.dma_start(pos_sb[0][:], pos1)
                     nc.sync.dma_start(pos_sb[1][:], pos2)
-                if e == last and o == 0:
-                    w2_first = load_w2(0)
-                is_end = e == last and o == PASSES - 1
-                n = e * PASSES + o
-                grouped = cast_w1(raw, SCALAR_M_LAST if is_end else (0 if n in VECTOR_CHUNKS else P))
-                gather_next(2 if n == 0 else 1)
-                wqs.append(quantize_w1(grouped))
+                if n in EARLY_W2:
+                    later[n] = cast_w2(EARLY_W2[n], later[n])
+                grouped = cast_w1(raw, SCALAR_SHARE[n])
+                gather_next(GATHERS[n])
+                wqs.append(quantize_w1(grouped, 4 if n == CHUNKS - 1 else 1))
                 if e > 0 and o == 0:
-                    planes = gelu_planes(banks)
+                    h_stage = gelu(banks)
                 if e > 0 and o == 1:
-                    h_grouped = interleave_h(planes)
+                    h_stage = interleave_h(h_stage)
                 if e > 0 and o == 2:
-                    quantize_h(e - 1, h_grouped)
-                if e == last and o == 2:
-                    layer2_product(0, layer2(0, w2_first, True))
-                first = PASSES - 1 if e == 0 else 0
+                    quantize_h(e - 1, h_stage)
+                if n in EARLY_W2:
+                    later[n] = layer2_product(EARLY_W2[n], quantize_w2(later[n]))
+                if n - 1 in EARLY_W2:
+                    copy_y(EARLY_W2[n - 1], later[n - 1], 0)
+                    copy_y(EARLY_W2[n - 1], later[n - 1], 1)
+                first = 0
                 if o == first:
-                    banks = [acc.tile([P, C], F32, name="acc") for t in range(PACK)]
+                    banks = open_banks()
                 if o >= first:
-                    for oo in (range(o + 1) if o == first else [o]):
-                        for t in range(PACK):
-                            layer1_pass(banks[t][:], e, oo, t, wqs[oo], slice(0, C))
+                    for oo in range(0 if o == first else o, o + 1):
+                        layer1_step(banks, e, oo, wqs[oo])
 
-        w2_raw = [load_w2(e) for e in range(1, E)]
+        late = range(len(EARLY_W2), E)
+        w2_raw = {e: load_w2(e) for e in late}
         gates = [load_gate(nt) for nt in range(N_TILES)]
 
-        quantize_h(last, interleave_h(gelu_planes(banks)))
-        for e in range(1, E):
-            layer2_product(e, layer2(e, w2_raw[e - 1], e == 1))
-
+        h_stage = gelu(banks)
+        quantize_h(last, interleave_h(h_stage))
+        ybanks = {}
+        for e in late:
+            ybanks[e] = layer2_product(e, quantize_w2(cast_w2(e, w2_raw[e])))
         for nt in range(N_TILES):
-            width = T if nt == 0 else T // 2
-            for t0 in range(0, T, width):
-                cols = slice(t0, t0 + width)
-                lst = slice(t0 // LIST_COLS, (t0 + width) // LIST_COLS)
-                prods = [stage.tile([P, width], F32, name="prod") for r in range(2)]
-                for r in range(2):
-                    nc.vector.tensor_tensor(prods[r][:], y_sb[nt][:].indirect(pos_sb[r][:, lst]), gates[nt][:, r, cols], MULT)
-                res = stage.tile([P, width], F32, name="res")
-                nc.vector.tensor_tensor(res[:], prods[0][:], prods[1][:], ADD)
-                nc.sync.dma_start(out=out[nt * P : (nt + 1) * P, cols], in_=res[:])
+            for e in late:
+                copy_y(e, ybanks[e], nt)
+
+        pieces = [[0,0,512],[1,0,384],[1,384,512]]
+        prods = []
+
+        def fetch(piece, r):
+            nt, t0, t1 = piece
+            prod = stage.tile([P, t1 - t0], F32, name="prod")
+            lst = pos_sb[r][:, t0 // LIST_COLS : t1 // LIST_COLS]
+            nc.vector.tensor_tensor(prod[:], y_sb[nt][:].indirect(lst), gates[nt][:, r, t0:t1], MULT)
+            return prod
+
+        def finish(piece, pair):
+            nt, t0, t1 = piece
+            res = stage.tile([P, t1 - t0], F32, name="res")
+            nc.vector.tensor_tensor(res[:], pair[0][:], pair[1][:], ADD)
+            nc.sync.dma_start(out=out[nt * P : (nt + 1) * P, t0:t1], in_=res[:])
+
+        for i, piece in enumerate(pieces):
+            first_prod = fetch(piece, 0)
+            if i > 0:
+                finish(pieces[i - 1], prods)
+            prods = [first_prod, fetch(piece, 1)]
+        finish(pieces[-1], prods)

@@ -20,276 +20,268 @@ P = 128
 PACK = 4
 K_PASS = P * PACK
 PASSES = K // K_PASS
+CHUNKS = E * PASSES
+QUADRANTS = 4
 PLANES = 4
 SLOTS = E * C
-HALF = 128
-N_TILES = N // P
-LIST_COLS = 16
+HALF = C // 2
 PAIR = 2 * C
-WINDOW = 768
-CHUNKS = E * PASSES
-SCALAR_SHARE = [128,128,128,128,0,128,128,0,128,128,0,128,0,128,0,128,0,80,44,44]
-W2_SHARE = [64,64,0,32]
-EARLY_W2 = {13:0}
-W2_TURN = {3:"after_matmul"}
-GATHERS = [1,1,1,1,1,1,1,1,1,1,1,1,1,1,1,1,1,1,1,1]
+WINDOW = T + T // 2
+N_TILES = N // P
+LIST_ROWS = 16
+
+RING = 10
+PLACE_BYTES = 4 * PACK * H
+
+SCALAR_ALONE = 10
+T_HALF = PACK // 2
+T_ORDER = (2, 3, 0, 1)
+GELU_AFTER = {7: 0, 11: 1, 16: 2}
+EARLY_W2 = {10: 0, 12: 1}
+Y_AFTER = 15
+LAST_SCALES_AT = 2
+POS_AT = 6
+LAST_PIECE = 128
 
 
 def tile_moe_pkd_mlp_gelu_kernel(tc, x_words, x_scales, w1, w2, gate, offs, pos1, pos2, out):
     nc = tc.nc
     with ExitStack() as ctx:
         keep = ctx.enter_context(tc.tile_pool(name="keep", bufs=1))
-        raws = ctx.enter_context(tc.tile_pool(name="raws", bufs=9))
+        ring = ctx.enter_context(tc.tile_pool(name="ring", bufs=1))
         stage = ctx.enter_context(tc.tile_pool(name="stage", bufs=4))
-        codes = ctx.enter_context(tc.tile_pool(name="codes", bufs=10))
+        codes = ctx.enter_context(tc.tile_pool(name="codes", bufs=2 * PASSES))
         turn = ctx.enter_context(tc.tile_pool(name="turn", bufs=1))
-        acc = ctx.enter_context(tc.psum_pool(name="acc", bufs=4))
-        yacc = ctx.enter_context(tc.psum_pool(name="yacc", bufs=4))
+        banks = ctx.enter_context(tc.psum_pool(name="banks", bufs=8))
 
-        offs_sb = keep.tile([P, SLOTS // LIST_COLS], U16, name="offs_sb")
-        pos_sb = [keep.tile([P, T // LIST_COLS], U16, name="pos_sb%d" % r) for r in range(2)]
-        tok_words = keep.tile([P, (PASSES - 1) * T + WINDOW], I32, name="tok_words", align_bytes=64)
-        tok_scales = keep.tile([P, 2, WINDOW], U8, name="tok_scales", align_bytes=64)
+        offs_sb = keep.tile([P, SLOTS // LIST_ROWS], U16, name="offs_sb")
+        pos_sb = [keep.tile([P, T // LIST_ROWS], U16, name="pos_sb%d" % r) for r in range(2)]
+        tok_words = [keep.tile([P, WINDOW], I32, name="tok_words%d" % o, align_bytes=64) for o in range(PASSES)]
+        tok_scales = [keep.tile([P, WINDOW], U8, name="tok_scales%d" % b, align_bytes=64) for b in range(2)]
         slot_words = [keep.tile([P, PASSES, PAIR], U32, name="slot_words%d" % g, align_bytes=64) for g in range(2)]
         slot_scales = [keep.tile([P, 2, PAIR], U8, name="slot_scales%d" % g, align_bytes=64) for g in range(2)]
         h_codes = [keep.tile([P, C], U32, name="h_codes%d" % e, align_bytes=64) for e in range(E)]
         h_scales = [keep.tile([P, C], U8, name="h_scales%d" % e, align_bytes=64) for e in range(E)]
-        y_sb = [keep.tile([P, SLOTS], F32, name="y_sb%d" % nt) for nt in range(N_TILES)]
+        y_sb = []
 
-        nc.vector.memset(tok_scales[:].rearrange("p b t -> p (b t)").bitcast(I32), 0)
-        nc.vector.memset(tok_words[:, PASSES * T :], 0)
+        places = list(range(RING))
+        filled = []
 
-        def load_scale_rows(d):
-            q = d % 4
-            if d < 4:
-                nc.sync.dma_start(
-                    out=tok_scales[32 * q : 32 * q + 16, 0, 0:T].bitcast(I32),
-                    in_=x_scales[0:PLANES, 4 * q : 4 * q + 4, :].bitcast(I32),
-                )
-            else:
-                nc.sync.dma_start(
-                    out=tok_scales[32 * q : 32 * q + 4, 1, 0:T].bitcast(I32),
-                    in_=x_scales[PLANES, 4 * q : 4 * q + 4, :].bitcast(I32),
-                )
+        def on_place(place, shape, dtype, name, skip):
+            return ring.tile(shape, dtype, name=name, align_bytes=64, offset=place * PLACE_BYTES + skip)
 
-        def load_words(o0, o1):
-            nc.sync.dma_start(
-                out=tok_words[:, o0 * T : o1 * T].rearrange("p (o t) -> p o t", t=T),
-                in_=x_words[o0:o1].rearrange("o p t r -> p o (t r)").bitcast(I32),
-            )
-
-        def load_w1(e, o):
-            raw = raws.tile([P, PACK, H], F32, name="raw")
-            nc.sync.dma_start(out=raw[:], in_=w1[e, o * K_PASS : (o + 1) * K_PASS, :].rearrange("(p j) i -> p j i", j=PACK))
+        def load(shape, src):
+            place = places.pop(0)
+            places.append(place)
+            filled.append(place)
+            raw = on_place(place, shape, F32, "raw%d" % len(filled), 0)
+            nc.sync.dma_start(out=raw[:], in_=src)
             return raw
+
+        def w1_rows(n):
+            e, o = divmod(n, PASSES)
+            return w1[e, o * K_PASS : (o + 1) * K_PASS, :].rearrange("(p j) i -> p j i", j=PACK)
 
         def load_w2(e):
-            raw = raws.tile([P, PACK, N], F32, name="raw")
-            nc.sync.dma_start(out=raw[:], in_=w2[e].rearrange("(p j) n -> p j n", j=PACK))
-            return raw
+            return load([P, PACK, N], w2[e].rearrange("(p j) n -> p j n", j=PACK))
 
-        def load_gate(nt):
-            raw = raws.tile([P, 2, T], F32, name="raw")
-            nc.sync.dma_start(out=raw[:], in_=gate[:, nt * P : (nt + 1) * P, :].rearrange("r p t -> p r t"))
-            return raw
-
-        def shared_cast(dst, src, split):
-            total = dst.shape[1]
-            if split > 0:
-                nc.scalar.copy(out=dst[:, 0:split], in_=src[:, 0:split])
-            if split < total:
-                nc.vector.tensor_copy(out=dst[:, split:total], in_=src[:, split:total])
-
-        def cast_w1(raw, split):
-            grouped = stage.tile([P, PACK, P, PACK], BF16, name="w1_grouped", align_bytes=64, bufs=8)
-            shared_cast(grouped[:].rearrange("p t m j -> p m j t"), raw[:].rearrange("p j (m t) -> p m j t", t=PACK), split)
-            return grouped
-
-        def quantize_w1(grouped, pieces):
-            pool, tag = (turn, "after_matmul") if pieces > 1 else (codes, "w1_codes")
-            wc = pool.tile([P, H], U32, name="w1_codes", tag=tag, align_bytes=64)
-            ws = codes.tile([P, H], U8, name="w1_scales", align_bytes=64)
-            flat = grouped[:].rearrange("p t m j -> p (t m j)")
-            width = H // pieces
-            for c0 in range(0, H, width):
-                nc.vector.quantize_mx(
-                    out=wc[:, c0 : c0 + width].bitcast(FP8X4),
-                    scales=ws[:, c0 : c0 + width],
-                    in_=flat[:, PACK * c0 : PACK * (c0 + width)],
+        def load_scale_rows(b):
+            o0, o1 = b * PLANES, min((b + 1) * PLANES, PASSES)
+            for q in range(QUADRANTS):
+                nc.sync.dma_start(
+                    out=tok_scales[b][32 * q : 32 * q + 4 * (o1 - o0), 0:T].bitcast(I32),
+                    in_=x_scales[o0:o1, 4 * q : 4 * q + 4, :].bitcast(I32),
                 )
-            return wc, ws
 
-        def gather(kind, g):
-            lst = offs_sb[:, g * (PAIR // LIST_COLS) : (g + 1) * (PAIR // LIST_COLS)]
-            if kind < PASSES:
-                window = tok_words[:, kind * T : kind * T + WINDOW].bitcast(U32)
-                nc.vector.tensor_copy(out=slot_words[g][:, kind, :], in_=window.indirect(lst))
-            else:
-                b = kind - PASSES
-                nc.vector.tensor_copy(out=slot_scales[g][:, b, :], in_=tok_scales[:, b, :].indirect(lst))
+        def pair_list(g):
+            return offs_sb[:, g * (PAIR // LIST_ROWS) : (g + 1) * (PAIR // LIST_ROWS)]
 
-        def layer1_pass(dst, e, o, t, wq, c0, c1, start, stop):
-            wc, ws = wq
-            first_row = 4 * (o % PLANES)
+        def gather_tokens(o):
+            for g in range(2):
+                nc.vector.tensor_copy(out=slot_words[g][:, o, :], in_=tok_words[o][:].bitcast(U32).indirect(pair_list(g)))
+                if o % PLANES == 0:
+                    b = o // PLANES
+                    nc.vector.tensor_copy(out=slot_scales[g][:, b, :], in_=tok_scales[b][:].indirect(pair_list(g)))
+
+        def round_w1(grouped, raw, j0, shared):
+            dst = grouped[:].rearrange("p t m j -> p m j t")[:, :, j0 : j0 + raw.shape[1], :]
+            src = raw[:].rearrange("p j (m t) -> p m j t", t=PACK)
+            split = T_HALF if shared else PACK
+            nc.scalar.copy(out=dst[:, :, :, 0:split], in_=src[:, :, :, 0:split])
+            if shared:
+                nc.vector.tensor_copy(out=dst[:, :, :, split:PACK], in_=src[:, :, :, split:PACK])
+
+        def quantize(words, scales, c0, c1, values):
+            nc.vector.quantize_mx(out=words[:, c0:c1].bitcast(FP8X4), scales=scales[:, c0:c1], in_=values)
+
+        def layer1_pass(pair, n, words, scales):
+            e, o = divmod(n, PASSES)
             g = e // 2
-            slots = slice((e % 2) * C + c0, (e % 2) * C + c1)
-            nc.tensor.matmul_mx(
-                out=dst,
-                lhsT=wc[:, t * P : (t + 1) * P].bitcast(FP8X4),
-                lhsT_scale=ws[:, t * P : (t + 1) * P],
-                rhs=slot_words[g][:, o, slots].bitcast(FP8X4),
-                rhs_scale=slot_scales[g][first_row:P, o // PLANES, slots],
-                start=start,
-                stop=stop,
-            )
+            for half in range(2):
+                slots = slice((e % 2) * C + half * HALF, (e % 2) * C + (half + 1) * HALF)
+                for t in T_ORDER:
+                    nc.tensor.matmul_mx(
+                        out=pair[half][:, t, :],
+                        lhsT=words[:, t * P : (t + 1) * P].bitcast(FP8X4),
+                        lhsT_scale=scales[:, t * P : (t + 1) * P],
+                        rhs=slot_words[g][:, o, slots].bitcast(FP8X4),
+                        rhs_scale=slot_scales[g][4 * (o % PLANES) : P, o // PLANES, slots],
+                        start=(o == 0 and t == T_ORDER[0]),
+                        stop=(o == PASSES - 1 and t == T_ORDER[-1]),
+                    )
 
-        def open_banks():
-            return [acc.tile([P, C], F32, name="acc") for t in range(PACK)]
+        def gelu(dst, bank):
+            nc.scalar.activation(out=dst, in_=bank[:].rearrange("p t s -> p s t"), func=GELU)
 
-        def layer1_step(banks, e, o, wq):
-            for t in range(PACK):
-                layer1_pass(banks[t][:], e, o, t, wq, 0, C, o == 0, o == PASSES - 1)
+        def quantize_h(e, s0, s1, h):
+            quantize(h_codes[e], h_scales[e], s0, s1, h[:].rearrange("p s t -> p (s t)"))
 
-        def gelu(banks):
-            planes = stage.tile([P, PACK, C], BF16, name="h_planes", bufs=2)
-            for t in range(PACK):
-                nc.scalar.activation(out=planes[:, t, :], in_=banks[t][:], func=GELU)
-            return planes
-
-        def interleave_h(planes):
-            grouped = stage.tile([P, C, PACK], BF16, name="h_grouped", align_bytes=64, bufs=2)
-            nc.vector.tensor_copy(
-                out=grouped[:].rearrange("p (c u) t -> p c t u", u=4), in_=planes[:].rearrange("p t (c u) -> p c t u", u=4)
+        def round_w2(copy, grouped, raw, n0):
+            n1 = n0 + grouped.shape[1]
+            copy(
+                out=grouped[:].rearrange("p (c u) j -> p c j u", u=4),
+                in_=raw[:, :, n0:n1].rearrange("p j (c u) -> p c j u", u=4),
             )
             return grouped
 
-        def quantize_h(e, grouped):
-            nc.vector.quantize_mx(
-                out=h_codes[e][:].bitcast(FP8X4), scales=h_scales[e][:], in_=grouped[:].rearrange("p c t -> p (c t)")
-            )
-
-        def cast_w2(e, raw):
-            pool, tag = (turn, W2_TURN[e]) if e in W2_TURN else (stage, "w2_grouped")
-            grouped = pool.tile([P, N, PACK], BF16, name="w2_grouped", tag=tag, align_bytes=64)
-            shared_cast(
-                grouped[:].rearrange("p (c u) j -> p c j u", u=4), raw[:].rearrange("p j (c u) -> p c j u", u=4), W2_SHARE[e]
-            )
-            return grouped
+        def w2_tile(width):
+            return stage.tile([P, width, PACK], BF16, name="w2_grouped", align_bytes=64)
 
         def quantize_w2(grouped):
-            wc = stage.tile([P, N], U32, name="w2_codes", align_bytes=64)
-            ws = stage.tile([P, N], U8, name="w2_scales", align_bytes=64)
-            nc.vector.quantize_mx(out=wc[:].bitcast(FP8X4), scales=ws[:], in_=grouped[:].rearrange("p n j -> p (n j)"))
-            return wc, ws
+            width = grouped.shape[1]
+            words = stage.tile([P, width], U32, name="w2_codes", align_bytes=64, bufs=6)
+            scales = stage.tile([P, width], U8, name="w2_scales", align_bytes=64, bufs=6)
+            quantize(words, scales, 0, width, grouped[:].rearrange("p n j -> p (n j)"))
+            return words, scales
 
-        def layer2_product(e, wq):
-            wc, ws = wq
-            if e == E - 1:
-                bank = [yacc.tile([P, C], F32, name="yacc")[:] for nt in range(N_TILES)]
-            else:
-                both = yacc.tile([P, N_TILES, C], F32, name="yacc")
-                bank = [both[:, nt, :] for nt in range(N_TILES)]
-            for nt in range(N_TILES):
-                nc.tensor.matmul_mx(
-                    out=bank[nt],
-                    lhsT=wc[:, nt * P : (nt + 1) * P].bitcast(FP8X4),
-                    lhsT_scale=ws[:, nt * P : (nt + 1) * P],
-                    rhs=h_codes[e][:].bitcast(FP8X4),
-                    rhs_scale=h_scales[e][:],
-                    start=True,
-                    stop=True,
-                )
-            return bank
+        def layer2_pass(dst, w2q, n0, e, s0, s1):
+            nc.tensor.matmul_mx(
+                out=dst,
+                lhsT=w2q[0][:, n0 : n0 + P].bitcast(FP8X4),
+                lhsT_scale=w2q[1][:, n0 : n0 + P],
+                rhs=h_codes[e][:, s0:s1].bitcast(FP8X4),
+                rhs_scale=h_scales[e][:, s0:s1],
+                start=True,
+                stop=True,
+            )
 
-        def copy_y(e, bank, nt):
-            nc.scalar.copy(out=y_sb[nt][:, e * C : (e + 1) * C], in_=bank[nt])
+        def late_y(nt, w2q, e, s0, s1):
+            bank = banks.tile([P, s1 - s0], F32, name="bank")
+            layer2_pass(bank[:], w2q, 0, e, s0, s1)
+            nc.scalar.copy(out=y_sb[nt][:, e * C + s0 : e * C + s1], in_=bank[:])
 
-        load_words(0, 2)
+        for b in range(2):
+            nc.vector.memset(tok_scales[b][:].bitcast(I32), 0)
+        for o in range(PASSES):
+            nc.vector.memset(tok_words[o][:, T:], 0)
         nc.sync.dma_start(offs_sb[:], offs)
-        for d in range(4):
-            load_scale_rows(d)
+
+        pairs = []
+        early_q = []
+        early_banks = []
+        for n in range(CHUNKS):
+            e, o = divmod(n, PASSES)
+            if e == 0:
+                nc.sync.dma_start(out=tok_words[o][:, 0:T], in_=x_words[o].rearrange("p t r -> p (t r)").bitcast(I32))
+            if n == 0:
+                raw = load([P, PACK, H], w1_rows(n))
+                load_scale_rows(0)
+            if n == LAST_SCALES_AT:
+                load_scale_rows(1)
+            if e == 0:
+                gather_tokens(o)
+            if n == POS_AT:
+                nc.sync.dma_start(pos_sb[0][:], pos1)
+                nc.sync.dma_start(pos_sb[1][:], pos2)
+            if n in EARLY_W2:
+                early = round_w2(nc.vector.tensor_copy, w2_tile(N), load_w2(EARLY_W2[n]), 0)
+
+            words = codes.tile([P, H], U32, name="w1_codes", align_bytes=64)
+            scales = codes.tile([P, H], U8, name="w1_scales", align_bytes=64)
+            if n < CHUNKS - 1:
+                if n > 0:
+                    raw = load([P, PACK, H], w1_rows(n))
+                grouped = stage.tile([P, PACK, P, PACK], BF16, name="w1_grouped", align_bytes=64, bufs=9)
+                round_w1(grouped, raw, 0, n >= SCALAR_ALONE)
+                quantize(words, scales, 0, H, grouped[:].rearrange("p t m j -> p (t m j)"))
+            else:
+                grouped = turn.tile([P, PACK, P, PACK], BF16, name="w1_last", tag="after_w1", align_bytes=64)
+                for j0 in (0, PACK // 2):
+                    round_w1(grouped, load([P, PACK // 2, H], w1_rows(n)[:, j0 : j0 + PACK // 2, :]), j0, True)
+                for t0 in (T_HALF, 0):
+                    share = grouped[:, t0 : t0 + T_HALF].rearrange("p t m j -> p (t m j)")
+                    quantize(words, scales, t0 * P, (t0 + T_HALF) * P, share)
+
+            if n - 1 in GELU_AFTER:
+                quantize_h(GELU_AFTER[n - 1], 0, C, h)
+            if n in GELU_AFTER:
+                h = on_place(filled[-1], [P, C, PACK], BF16, "h%d" % n, 0)
+                for half in range(2):
+                    gelu(h[:, half * HALF : (half + 1) * HALF, :], pairs[GELU_AFTER[n]][half])
+            if n in EARLY_W2:
+                early_q.append(quantize_w2(early))
+            if n == Y_AFTER - 1:
+                for nt in range(N_TILES):
+                    early_banks.append(banks.tile([P, len(EARLY_W2), C], F32, name="bank"))
+                    for i, w2q in enumerate(early_q):
+                        layer2_pass(early_banks[nt][:, i, :], w2q, nt * P, i, 0, C)
+            if n == Y_AFTER:
+                places.remove(filled[-1])
+                for nt in range(N_TILES):
+                    y_sb.append(on_place(filled[-1], [P, SLOTS], F32, "y_sb%d" % nt, nt * 4 * SLOTS))
+                    nc.scalar.copy(
+                        out=y_sb[nt][:, 0 : len(EARLY_W2) * C], in_=early_banks[nt][:].rearrange("p i c -> p (i c)")
+                    )
+            if o == 0:
+                pairs.append([banks.tile([P, PACK, HALF], F32, name="bank") for half in range(2)])
+            layer1_pass(pairs[e], n, words, scales)
+
         last = E - 1
-        pending = [(0, 0), (5, 0), (0, 1), (1, 0), (2, 0), (3, 0), (4, 0), (6, 0), (5, 1), (1, 1), (2, 1), (3, 1), (4, 1), (6, 1)]
-        later = {}
+        raw_last = load_w2(last)
+        raw_late = load_w2(last - 1)
+        gates = load([P, 2, T], gate[:, 0:P, :].rearrange("r p t -> p r t"))
 
-        def gather_next(count):
-            for kind, g in pending[0:count]:
-                gather(kind, g)
-                pending.remove((kind, g))
-
-        gather_next(3)
-        banks = []
-        h_stage = None
-        for e in range(E):
-            wqs = []
-            for o in range(PASSES):
-                n = e * PASSES + o
-                if n in EARLY_W2:
-                    later[n] = load_w2(EARLY_W2[n])
-                raw = load_w1(e, o)
-                if n == 0:
-                    load_words(2, PASSES)
-                if n == 0:
-                    for d in range(4, 8):
-                        load_scale_rows(d)
-                if n == 5:
-                    nc.sync.dma_start(pos_sb[0][:], pos1)
-                    nc.sync.dma_start(pos_sb[1][:], pos2)
-                if n in EARLY_W2:
-                    later[n] = cast_w2(EARLY_W2[n], later[n])
-                grouped = cast_w1(raw, SCALAR_SHARE[n])
-                gather_next(GATHERS[n])
-                wqs.append(quantize_w1(grouped, 4 if n == CHUNKS - 1 else 1))
-                if e > 0 and o == 0:
-                    h_stage = gelu(banks)
-                if e > 0 and o == 1:
-                    h_stage = interleave_h(h_stage)
-                if e > 0 and o == 2:
-                    quantize_h(e - 1, h_stage)
-                if n in EARLY_W2:
-                    later[n] = layer2_product(EARLY_W2[n], quantize_w2(later[n]))
-                if n - 1 in EARLY_W2:
-                    copy_y(EARLY_W2[n - 1], later[n - 1], 0)
-                    copy_y(EARLY_W2[n - 1], later[n - 1], 1)
-                first = 0
-                if o == first:
-                    banks = open_banks()
-                if o >= first:
-                    for oo in range(0 if o == first else o, o + 1):
-                        layer1_step(banks, e, oo, wqs[oo])
-
-        late = range(len(EARLY_W2), E)
-        w2_raw = {e: load_w2(e) for e in late}
-        gates = [load_gate(nt) for nt in range(N_TILES)]
-
-        h_stage = gelu(banks)
-        quantize_h(last, interleave_h(h_stage))
-        ybanks = {}
-        for e in late:
-            ybanks[e] = layer2_product(e, quantize_w2(cast_w2(e, w2_raw[e])))
-        for nt in range(N_TILES):
-            for e in late:
-                copy_y(e, ybanks[e], nt)
-
-        pieces = [[0,0,512],[1,0,384],[1,384,512]]
-        prods = []
+        behind_w1 = turn.tile([P, P, PACK], BF16, name="w2_behind_w1", tag="after_w1", align_bytes=64)
+        last_rounded = [
+            round_w2(nc.scalar.copy, w2_tile(P), raw_last, 0),
+            round_w2(nc.vector.tensor_copy, behind_w1, raw_last, P),
+        ]
+        h_halves = [
+            stage.tile([P, HALF, PACK], BF16, name="h_first", align_bytes=64, bufs=1),
+            turn.tile([P, HALF, PACK], BF16, name="h_second", tag="after_h", align_bytes=64),
+        ]
+        for half in range(2):
+            gelu(h_halves[half][:], pairs[last][half])
+        last_q = [quantize_w2(rounded) for rounded in last_rounded]
+        late_rounded = round_w2(nc.vector.tensor_copy, w2_tile(P), raw_late, 0)
+        quantize_h(last, 0, HALF, h_halves[0])
+        late_q = [quantize_w2(late_rounded)]
+        quantize_h(last, HALF, C, h_halves[1])
+        behind_h = turn.tile([P, P, PACK], BF16, name="w2_behind_h", tag="after_h", align_bytes=64)
+        late_q.append(quantize_w2(round_w2(nc.vector.tensor_copy, behind_h, raw_late, P)))
+        late_y(0, last_q[0], last, 0, HALF)
+        late_y(0, late_q[0], last - 1, 0, C)
+        late_y(0, last_q[0], last, HALF, C)
+        late_y(1, last_q[1], last, 0, C)
+        late_y(1, late_q[1], last - 1, 0, C)
 
         def fetch(piece, r):
             nt, t0, t1 = piece
             prod = stage.tile([P, t1 - t0], F32, name="prod")
-            lst = pos_sb[r][:, t0 // LIST_COLS : t1 // LIST_COLS]
-            nc.vector.tensor_tensor(prod[:], y_sb[nt][:].indirect(lst), gates[nt][:, r, t0:t1], MULT)
+            entries = pos_sb[r][:, t0 // LIST_ROWS : t1 // LIST_ROWS]
+            nc.vector.tensor_tensor(prod[:], y_sb[nt][:].indirect(entries), gates[:, r, t0:t1], MULT)
             return prod
 
-        def finish(piece, pair):
+        def finish(piece, prods):
             nt, t0, t1 = piece
-            res = stage.tile([P, t1 - t0], F32, name="res")
-            nc.vector.tensor_tensor(res[:], pair[0][:], pair[1][:], ADD)
+            res = stage.tile([P, t1 - t0], F32, name="res", bufs=3)
+            nc.vector.tensor_tensor(res[:], prods[0][:], prods[1][:], ADD)
             nc.sync.dma_start(out=out[nt * P : (nt + 1) * P, t0:t1], in_=res[:])
 
-        for i, piece in enumerate(pieces):
-            first_prod = fetch(piece, 0)
-            if i > 0:
-                finish(pieces[i - 1], prods)
-            prods = [first_prod, fetch(piece, 1)]
+        pieces = [(0, 0, T), (1, 0, T - LAST_PIECE), (1, T - LAST_PIECE, T)]
+        prods = [fetch(pieces[0], 0), fetch(pieces[0], 1)]
+        for before, piece in zip(pieces, pieces[1:]):
+            first = fetch(piece, 0)
+            finish(before, prods)
+            prods = [first, fetch(piece, 1)]
         finish(pieces[-1], prods)

@@ -1,6 +1,7 @@
 from contextlib import ExitStack
 
 import concourse.mybir as mybir
+from concourse.masks import make_identity
 
 K, T, E, C, H, N = 2560, 512, 4, 256, 512, 256
 FLOPS = 2 * E * C * (K * H + H * N)
@@ -37,8 +38,7 @@ SCALAR_ALONE = 10
 T_HALF = PACK // 2
 T_ORDER = (2, 3, 0, 1)
 GELU_AFTER = {7: 0, 11: 1, 16: 2}
-EARLY_W2 = {10: 0, 12: 1}
-Y_AFTER = 15
+EARLY_W2_AT = 12
 LAST_SCALES_AT = 2
 POS_AT = 6
 LAST_PIECE = 128
@@ -62,7 +62,7 @@ def tile_moe_pkd_mlp_gelu_kernel(tc, x_words, x_scales, w1, w2, gate, offs, pos1
         slot_scales = [keep.tile([P, 2, PAIR], U8, name="slot_scales%d" % g, align_bytes=64) for g in range(2)]
         h_codes = [keep.tile([P, C], U32, name="h_codes%d" % e, align_bytes=64) for e in range(E)]
         h_scales = [keep.tile([P, C], U8, name="h_scales%d" % e, align_bytes=64) for e in range(E)]
-        y_sb = []
+        y_sb = [keep.tile([P, SLOTS], F32, name="y_sb%d" % nt) for nt in range(N_TILES)]
 
         places = list(range(RING))
         filled = []
@@ -82,8 +82,8 @@ def tile_moe_pkd_mlp_gelu_kernel(tc, x_words, x_scales, w1, w2, gate, offs, pos1
             e, o = divmod(n, PASSES)
             return w1[e, o * K_PASS : (o + 1) * K_PASS, :].rearrange("(p j) i -> p j i", j=PACK)
 
-        def load_w2(e):
-            return load([P, PACK, N], w2[e].rearrange("(p j) n -> p j n", j=PACK))
+        def load_w2(e, n0, n1):
+            return load([P, PACK, n1 - n0], w2[e, :, n0:n1].rearrange("(p j) n -> p j n", j=PACK))
 
         def load_scale_rows(b):
             o0, o1 = b * PLANES, min((b + 1) * PLANES, PASSES)
@@ -149,8 +149,8 @@ def tile_moe_pkd_mlp_gelu_kernel(tc, x_words, x_scales, w1, w2, gate, offs, pos1
 
         def quantize_w2(grouped):
             width = grouped.shape[1]
-            words = stage.tile([P, width], U32, name="w2_codes", align_bytes=64, bufs=6)
-            scales = stage.tile([P, width], U8, name="w2_scales", align_bytes=64, bufs=6)
+            words = stage.tile([P, width], U32, name="w2_codes", align_bytes=64, bufs=7)
+            scales = stage.tile([P, width], U8, name="w2_scales", align_bytes=64, bufs=7)
             quantize(words, scales, 0, width, grouped[:].rearrange("p n j -> p (n j)"))
             return words, scales
 
@@ -165,20 +165,20 @@ def tile_moe_pkd_mlp_gelu_kernel(tc, x_words, x_scales, w1, w2, gate, offs, pos1
                 stop=True,
             )
 
-        def late_y(nt, w2q, e, s0, s1):
+        def late_y(nt, w2q, e, s0, s1, n0=0):
             bank = banks.tile([P, s1 - s0], F32, name="bank")
-            layer2_pass(bank[:], w2q, 0, e, s0, s1)
+            layer2_pass(bank[:], w2q, n0, e, s0, s1)
             nc.scalar.copy(out=y_sb[nt][:, e * C + s0 : e * C + s1], in_=bank[:])
 
         for b in range(2):
             nc.vector.memset(tok_scales[b][:].bitcast(I32), 0)
         for o in range(PASSES):
             nc.vector.memset(tok_words[o][:, T:], 0)
+        identity = keep.tile([P, P], F32, name="identity")
+        make_identity(nc, identity[:])
         nc.sync.dma_start(offs_sb[:], offs)
 
         pairs = []
-        early_q = []
-        early_banks = []
         for n in range(CHUNKS):
             e, o = divmod(n, PASSES)
             if e == 0:
@@ -193,8 +193,8 @@ def tile_moe_pkd_mlp_gelu_kernel(tc, x_words, x_scales, w1, w2, gate, offs, pos1
             if n == POS_AT:
                 nc.sync.dma_start(pos_sb[0][:], pos1)
                 nc.sync.dma_start(pos_sb[1][:], pos2)
-            if n in EARLY_W2:
-                early = round_w2(nc.vector.tensor_copy, w2_tile(N), load_w2(EARLY_W2[n]), 0)
+            if n == EARLY_W2_AT:
+                early = round_w2(nc.vector.tensor_copy, w2_tile(N), load_w2(E - 1, 0, N), 0)
 
             words = codes.tile([P, H], U32, name="w1_codes", align_bytes=64)
             scales = codes.tile([P, H], U8, name="w1_scales", align_bytes=64)
@@ -218,33 +218,24 @@ def tile_moe_pkd_mlp_gelu_kernel(tc, x_words, x_scales, w1, w2, gate, offs, pos1
                 h = on_place(filled[-1], [P, C, PACK], BF16, "h%d" % n, 0)
                 for half in range(2):
                     gelu(h[:, half * HALF : (half + 1) * HALF, :], pairs[GELU_AFTER[n]][half])
-            if n in EARLY_W2:
-                early_q.append(quantize_w2(early))
-            if n == Y_AFTER - 1:
-                for nt in range(N_TILES):
-                    early_banks.append(banks.tile([P, len(EARLY_W2), C], F32, name="bank"))
-                    for i, w2q in enumerate(early_q):
-                        layer2_pass(early_banks[nt][:, i, :], w2q, nt * P, i, 0, C)
-            if n == Y_AFTER:
-                places.remove(filled[-1])
-                for nt in range(N_TILES):
-                    y_sb.append(on_place(filled[-1], [P, SLOTS], F32, "y_sb%d" % nt, nt * 4 * SLOTS))
-                    nc.scalar.copy(
-                        out=y_sb[nt][:, 0 : len(EARLY_W2) * C], in_=early_banks[nt][:].rearrange("p i c -> p (i c)")
-                    )
+            if n == EARLY_W2_AT:
+                last_q = quantize_w2(early)
             if o == 0:
                 pairs.append([banks.tile([P, PACK, HALF], F32, name="bank") for half in range(2)])
             layer1_pass(pairs[e], n, words, scales)
 
         last = E - 1
-        raw_last = load_w2(last)
-        raw_late = load_w2(last - 1)
-        gates = load([P, 2, T], gate[:, 0:P, :].rearrange("r p t -> p r t"))
+        raw_a = load_w2(2, 0, N)
+        raw_b = load_w2(1, 0, N)
+        raw_c = [load_w2(0, nt * P, (nt + 1) * P) for nt in range(N_TILES)]
+        gates = [load([P, T], gate[r, 0:P, :]) for r in range(2)]
 
-        behind_w1 = turn.tile([P, P, PACK], BF16, name="w2_behind_w1", tag="after_w1", align_bytes=64)
-        last_rounded = [
-            round_w2(nc.scalar.copy, w2_tile(P), raw_last, 0),
-            round_w2(nc.vector.tensor_copy, behind_w1, raw_last, P),
+        def in_turn(tag):
+            return turn.tile([P, P, PACK], BF16, name="w2_" + tag, tag=tag, align_bytes=64)
+
+        a_rounded = [
+            round_w2(nc.scalar.copy, w2_tile(P), raw_a, 0),
+            round_w2(nc.vector.tensor_copy, in_turn("after_w1"), raw_a, P),
         ]
         h_halves = [
             stage.tile([P, HALF, PACK], BF16, name="h_first", align_bytes=64, bufs=1),
@@ -252,36 +243,66 @@ def tile_moe_pkd_mlp_gelu_kernel(tc, x_words, x_scales, w1, w2, gate, offs, pos1
         ]
         for half in range(2):
             gelu(h_halves[half][:], pairs[last][half])
-        last_q = [quantize_w2(rounded) for rounded in last_rounded]
-        late_rounded = round_w2(nc.vector.tensor_copy, w2_tile(P), raw_late, 0)
+        a_q = [quantize_w2(rounded) for rounded in a_rounded]
+        c_rounded = round_w2(nc.scalar.copy, in_turn("after_w1"), raw_c[0], 0)
+        b_rounded = round_w2(nc.vector.tensor_copy, w2_tile(P), raw_b, 0)
         quantize_h(last, 0, HALF, h_halves[0])
-        late_q = [quantize_w2(late_rounded)]
+        b_q = [quantize_w2(b_rounded)]
         quantize_h(last, HALF, C, h_halves[1])
-        behind_h = turn.tile([P, P, PACK], BF16, name="w2_behind_h", tag="after_h", align_bytes=64)
-        late_q.append(quantize_w2(round_w2(nc.vector.tensor_copy, behind_h, raw_late, P)))
-        late_y(0, last_q[0], last, 0, HALF)
-        late_y(0, late_q[0], last - 1, 0, C)
-        late_y(0, last_q[0], last, HALF, C)
-        late_y(1, last_q[1], last, 0, C)
-        late_y(1, late_q[1], last - 1, 0, C)
+        c_q = [quantize_w2(c_rounded)]
+        b_q.append(quantize_w2(round_w2(nc.vector.tensor_copy, in_turn("after_h"), raw_b, P)))
+        c_q.append(quantize_w2(round_w2(nc.vector.tensor_copy, in_turn("after_h"), raw_c[1], 0)))
+        late_y(0, a_q[0], 2, 0, C)
+        late_y(0, last_q, last, 0, HALF)
+        late_y(0, b_q[0], 1, 0, C)
+        late_y(0, last_q, last, HALF, C)
+        late_y(0, c_q[0], 0, 0, C)
+        late_y(1, a_q[1], 2, 0, C)
+        late_y(1, last_q, last, 0, C, P)
+        late_y(1, b_q[1], 1, 0, C)
+        late_y(1, c_q[1], 0, 0, C)
 
         def fetch(piece, r):
             nt, t0, t1 = piece
-            prod = stage.tile([P, t1 - t0], F32, name="prod")
+            prod = stage.tile([P, t1 - t0], F32, name="prod", bufs=8)
             entries = pos_sb[r][:, t0 // LIST_ROWS : t1 // LIST_ROWS]
-            nc.vector.tensor_tensor(prod[:], y_sb[nt][:].indirect(entries), gates[:, r, t0:t1], MULT)
+            nc.vector.tensor_tensor(prod[:], y_sb[nt][:].indirect(entries), gates[r][:, t0:t1], MULT)
             return prod
 
         def finish(piece, prods):
             nt, t0, t1 = piece
-            res = stage.tile([P, t1 - t0], F32, name="res", bufs=3)
+            res = stage.tile([P, t1 - t0], F32, name="res", bufs=4)
             nc.vector.tensor_tensor(res[:], prods[0][:], prods[1][:], ADD)
             nc.sync.dma_start(out=out[nt * P : (nt + 1) * P, t0:t1], in_=res[:])
 
-        pieces = [(0, 0, T), (1, 0, T - LAST_PIECE), (1, T - LAST_PIECE, T)]
-        prods = [fetch(pieces[0], 0), fetch(pieces[0], 1)]
-        for before, piece in zip(pieces, pieces[1:]):
-            first = fetch(piece, 0)
-            finish(before, prods)
-            prods = [first, fetch(piece, 1)]
-        finish(pieces[-1], prods)
+        def turn_blocks(bank, src, start, stop):
+            for b in range(2):
+                nc.tensor.matmul(
+                    out=bank[:, b, :],
+                    lhsT=src[:, b * P : (b + 1) * P],
+                    rhs=identity[:],
+                    is_transpose=True,
+                    start=start and b == 0,
+                    stop=stop and b == 1,
+                )
+
+        def finish_on_tensor(piece, prods):
+            nt, t0, t1 = piece
+            sums = banks.tile([P, 2, P], F32, name="bank")
+            for r in range(2):
+                turn_blocks(sums, prods[r], r == 0, r == 1)
+            turned = stage.tile([P, 2 * P], F32, name="turned", bufs=2)
+            nc.scalar.copy(out=turned[:], in_=sums[:].rearrange("p b n -> p (b n)"))
+            back = banks.tile([P, 2, P], F32, name="bank")
+            turn_blocks(back, turned, True, True)
+            res = stage.tile([P, 2 * P], F32, name="res", bufs=4)
+            nc.scalar.copy(out=res[:], in_=back[:].rearrange("p b n -> p (b n)"))
+            nc.sync.dma_start(out=out[nt * P : (nt + 1) * P, t0:t1], in_=res[:])
+
+        for piece in ((0, 0, T // 2), (0, T // 2, T)):
+            finish_on_tensor(piece, [fetch(piece, 0), fetch(piece, 1)])
+        wide, narrow = (1, 0, T - LAST_PIECE), (1, T - LAST_PIECE, T)
+        prods = [fetch(wide, 0), fetch(wide, 1)]
+        first = fetch(narrow, 0)
+        finish(wide, prods)
+        finish(narrow, [first, fetch(narrow, 1)])

@@ -38,7 +38,7 @@ SCALAR_ALONE = 10
 T_HALF = PACK // 2
 T_ORDER = (2, 3, 0, 1)
 GELU_AFTER = {7: 0, 11: 1, 16: 2}
-EARLY_W2_AT = 12
+LAST_W2_AT = 12
 LAST_SCALES_AT = 2
 POS_AT = 6
 LAST_PIECE = 128
@@ -52,7 +52,8 @@ def tile_moe_pkd_mlp_gelu_kernel(tc, x_words, x_scales, w1, w2, gate, offs, pos1
         stage = ctx.enter_context(tc.tile_pool(name="stage", bufs=4))
         codes = ctx.enter_context(tc.tile_pool(name="codes", bufs=2 * PASSES))
         turn = ctx.enter_context(tc.tile_pool(name="turn", bufs=1))
-        banks = ctx.enter_context(tc.psum_pool(name="banks", bufs=8))
+        banks = ctx.enter_context(tc.psum_pool(name="banks", bufs=7))
+        turn_bank = ctx.enter_context(tc.psum_pool(name="turn_bank", bufs=1))
 
         offs_sb = keep.tile([P, SLOTS // LIST_ROWS], U16, name="offs_sb")
         pos_sb = [keep.tile([P, T // LIST_ROWS], U16, name="pos_sb%d" % r) for r in range(2)]
@@ -154,21 +155,22 @@ def tile_moe_pkd_mlp_gelu_kernel(tc, x_words, x_scales, w1, w2, gate, offs, pos1
             quantize(words, scales, 0, width, grouped[:].rearrange("p n j -> p (n j)"))
             return words, scales
 
-        def layer2_pass(dst, w2q, n0, e, s0, s1):
-            nc.tensor.matmul_mx(
-                out=dst,
-                lhsT=w2q[0][:, n0 : n0 + P].bitcast(FP8X4),
-                lhsT_scale=w2q[1][:, n0 : n0 + P],
-                rhs=h_codes[e][:, s0:s1].bitcast(FP8X4),
-                rhs_scale=h_scales[e][:, s0:s1],
-                start=True,
-                stop=True,
-            )
-
-        def late_y(nt, w2q, e, s0, s1, n0=0):
-            bank = banks.tile([P, s1 - s0], F32, name="bank")
-            layer2_pass(bank[:], w2q, n0, e, s0, s1)
-            nc.scalar.copy(out=y_sb[nt][:, e * C + s0 : e * C + s1], in_=bank[:])
+        def make_y(pool, nt, parts):
+            first_slot = parts[0][2] * C + parts[0][3]
+            width = sum(s1 - s0 for w2q, n0, e, s0, s1 in parts)
+            bank = pool.tile([P, width], F32, name="bank")
+            for w2q, n0, e, s0, s1 in parts:
+                c0 = e * C + s0 - first_slot
+                nc.tensor.matmul_mx(
+                    out=bank[:, c0 : c0 + s1 - s0],
+                    lhsT=w2q[0][:, n0 : n0 + P].bitcast(FP8X4),
+                    lhsT_scale=w2q[1][:, n0 : n0 + P],
+                    rhs=h_codes[e][:, s0:s1].bitcast(FP8X4),
+                    rhs_scale=h_scales[e][:, s0:s1],
+                    start=True,
+                    stop=True,
+                )
+            nc.scalar.copy(out=y_sb[nt][:, first_slot : first_slot + width], in_=bank[:])
 
         for b in range(2):
             nc.vector.memset(tok_scales[b][:].bitcast(I32), 0)
@@ -178,6 +180,7 @@ def tile_moe_pkd_mlp_gelu_kernel(tc, x_words, x_scales, w1, w2, gate, offs, pos1
         make_identity(nc, identity[:])
         nc.sync.dma_start(offs_sb[:], offs)
 
+        last = E - 1
         pairs = []
         for n in range(CHUNKS):
             e, o = divmod(n, PASSES)
@@ -193,8 +196,8 @@ def tile_moe_pkd_mlp_gelu_kernel(tc, x_words, x_scales, w1, w2, gate, offs, pos1
             if n == POS_AT:
                 nc.sync.dma_start(pos_sb[0][:], pos1)
                 nc.sync.dma_start(pos_sb[1][:], pos2)
-            if n == EARLY_W2_AT:
-                early = round_w2(nc.vector.tensor_copy, w2_tile(N), load_w2(E - 1, 0, N), 0)
+            if n == LAST_W2_AT:
+                last_rounded = round_w2(nc.vector.tensor_copy, w2_tile(N), load_w2(last, 0, N), 0)
 
             words = codes.tile([P, H], U32, name="w1_codes", align_bytes=64)
             scales = codes.tile([P, H], U8, name="w1_scales", align_bytes=64)
@@ -218,24 +221,23 @@ def tile_moe_pkd_mlp_gelu_kernel(tc, x_words, x_scales, w1, w2, gate, offs, pos1
                 h = on_place(filled[-1], [P, C, PACK], BF16, "h%d" % n, 0)
                 for half in range(2):
                     gelu(h[:, half * HALF : (half + 1) * HALF, :], pairs[GELU_AFTER[n]][half])
-            if n == EARLY_W2_AT:
-                last_q = quantize_w2(early)
+            if n == LAST_W2_AT:
+                last_q = quantize_w2(last_rounded)
             if o == 0:
                 pairs.append([banks.tile([P, PACK, HALF], F32, name="bank") for half in range(2)])
             layer1_pass(pairs[e], n, words, scales)
 
-        last = E - 1
-        raw_a = load_w2(2, 0, N)
-        raw_b = load_w2(1, 0, N)
-        raw_c = [load_w2(0, nt * P, (nt + 1) * P) for nt in range(N_TILES)]
+        raw2 = load_w2(2, 0, N)
+        raw1 = load_w2(1, 0, N)
+        raw0 = [load_w2(0, nt * P, (nt + 1) * P) for nt in range(N_TILES)]
         gates = [load([P, T], gate[r, 0:P, :]) for r in range(2)]
 
         def in_turn(tag):
             return turn.tile([P, P, PACK], BF16, name="w2_" + tag, tag=tag, align_bytes=64)
 
-        a_rounded = [
-            round_w2(nc.scalar.copy, w2_tile(P), raw_a, 0),
-            round_w2(nc.vector.tensor_copy, in_turn("after_w1"), raw_a, P),
+        rounded2 = [
+            round_w2(nc.scalar.copy, w2_tile(P), raw2, 0),
+            round_w2(nc.vector.tensor_copy, in_turn("after_w1"), raw2, P),
         ]
         h_halves = [
             stage.tile([P, HALF, PACK], BF16, name="h_first", align_bytes=64, bufs=1),
@@ -243,24 +245,21 @@ def tile_moe_pkd_mlp_gelu_kernel(tc, x_words, x_scales, w1, w2, gate, offs, pos1
         ]
         for half in range(2):
             gelu(h_halves[half][:], pairs[last][half])
-        a_q = [quantize_w2(rounded) for rounded in a_rounded]
-        c_rounded = round_w2(nc.scalar.copy, in_turn("after_w1"), raw_c[0], 0)
-        b_rounded = round_w2(nc.vector.tensor_copy, w2_tile(P), raw_b, 0)
+        q2 = [quantize_w2(rounded) for rounded in rounded2]
+        rounded0 = round_w2(nc.scalar.copy, in_turn("after_w1"), raw0[0], 0)
+        rounded1 = round_w2(nc.vector.tensor_copy, w2_tile(P), raw1, 0)
         quantize_h(last, 0, HALF, h_halves[0])
-        b_q = [quantize_w2(b_rounded)]
+        q1 = [quantize_w2(rounded1)]
         quantize_h(last, HALF, C, h_halves[1])
-        c_q = [quantize_w2(c_rounded)]
-        b_q.append(quantize_w2(round_w2(nc.vector.tensor_copy, in_turn("after_h"), raw_b, P)))
-        c_q.append(quantize_w2(round_w2(nc.vector.tensor_copy, in_turn("after_h"), raw_c[1], 0)))
-        late_y(0, a_q[0], 2, 0, C)
-        late_y(0, last_q, last, 0, HALF)
-        late_y(0, b_q[0], 1, 0, C)
-        late_y(0, last_q, last, HALF, C)
-        late_y(0, c_q[0], 0, 0, C)
-        late_y(1, a_q[1], 2, 0, C)
-        late_y(1, last_q, last, 0, C, P)
-        late_y(1, b_q[1], 1, 0, C)
-        late_y(1, c_q[1], 0, 0, C)
+        q0 = [quantize_w2(rounded0)]
+        q1.append(quantize_w2(round_w2(nc.vector.tensor_copy, in_turn("after_h"), raw1, P)))
+        q0.append(quantize_w2(round_w2(nc.vector.tensor_copy, in_turn("after_h"), raw0[1], 0)))
+        make_y(banks, 0, [(q1[0], 0, 1, 0, C), (q2[0], 0, 2, 0, C)])
+        make_y(banks, 0, [(last_q, 0, last, 0, HALF)])
+        make_y(banks, 0, [(last_q, 0, last, HALF, C)])
+        make_y(turn_bank, 0, [(q0[0], 0, 0, 0, C)])
+        make_y(turn_bank, 1, [(q2[1], 0, 2, 0, C), (last_q, P, last, 0, C)])
+        make_y(banks, 1, [(q0[1], 0, 0, 0, C), (q1[1], 0, 1, 0, C)])
 
         def fetch(piece, r):
             nt, t0, t1 = piece

@@ -245,15 +245,19 @@ def tile_moe_pkd_mlp_gelu_kernel(tc, x_words, x_scales, w1, w2, gate, offs, pos1
         ]
         for half in range(2):
             gelu(h_halves[half][:], pairs[last][half])
-        q2 = [quantize_w2(rounded) for rounded in rounded2]
-        rounded0 = round_w2(nc.scalar.copy, in_turn("after_w1"), raw0[0], 0)
+        q2 = [quantize_w2(rounded2[0])]
         rounded1 = round_w2(nc.vector.tensor_copy, w2_tile(P), raw1, 0)
-        quantize_h(last, 0, HALF, h_halves[0])
+        q2.append(quantize_w2(rounded2[1]))
         q1 = [quantize_w2(rounded1)]
+        quantize_h(last, 0, HALF, h_halves[0])
+        rounded0 = round_w2(nc.vector.tensor_copy, in_turn("after_w1"), raw0[0], 0)
         quantize_h(last, HALF, C, h_halves[1])
         q0 = [quantize_w2(rounded0)]
-        q1.append(quantize_w2(round_w2(nc.vector.tensor_copy, in_turn("after_h"), raw1, P)))
-        q0.append(quantize_w2(round_w2(nc.vector.tensor_copy, in_turn("after_h"), raw0[1], 0)))
+        both = turn.tile([P, N, PACK], BF16, name="w2_both", tag="after_h", align_bytes=64)
+        round_w2(nc.vector.tensor_copy, both[:, 0:P], raw1, P)
+        round_w2(nc.vector.tensor_copy, both[:, P:N], raw0[1], 0)
+        q1.append(quantize_w2(both[:, 0:P]))
+        q0.append(quantize_w2(both[:, P:N]))
         make_y(banks, 0, [(q1[0], 0, 1, 0, C), (q2[0], 0, 2, 0, C)])
         make_y(banks, 0, [(last_q, 0, last, 0, HALF)])
         make_y(banks, 0, [(last_q, 0, last, HALF, C)])
@@ -261,17 +265,14 @@ def tile_moe_pkd_mlp_gelu_kernel(tc, x_words, x_scales, w1, w2, gate, offs, pos1
         make_y(turn_bank, 1, [(q2[1], 0, 2, 0, C), (last_q, P, last, 0, C)])
         make_y(banks, 1, [(q0[1], 0, 0, 0, C), (q1[1], 0, 1, 0, C)])
 
-        def fetch(piece, r):
-            nt, t0, t1 = piece
-            prod = stage.tile([P, t1 - t0], F32, name="prod", bufs=8)
-            entries = pos_sb[r][:, t0 // LIST_ROWS : t1 // LIST_ROWS]
-            nc.vector.tensor_tensor(prod[:], y_sb[nt][:].indirect(entries), gates[r][:, t0:t1], MULT)
+        def fetch(nt, r):
+            prod = stage.tile([P, T], F32, name="prod", bufs=4)
+            nc.vector.tensor_tensor(prod[:], y_sb[nt][:].indirect(pos_sb[r][:]), gates[r][:], MULT)
             return prod
 
-        def finish(piece, prods):
-            nt, t0, t1 = piece
+        def finish(nt, t0, t1, prods):
             res = stage.tile([P, t1 - t0], F32, name="res", bufs=4)
-            nc.vector.tensor_tensor(res[:], prods[0][:], prods[1][:], ADD)
+            nc.vector.tensor_tensor(res[:], prods[0][:, t0:t1], prods[1][:, t0:t1], ADD)
             nc.sync.dma_start(out=out[nt * P : (nt + 1) * P, t0:t1], in_=res[:])
 
         def turn_blocks(bank, src, start, stop):
@@ -285,23 +286,23 @@ def tile_moe_pkd_mlp_gelu_kernel(tc, x_words, x_scales, w1, w2, gate, offs, pos1
                     stop=stop and b == 1,
                 )
 
-        def finish_on_tensor(piece, prods):
-            nt, t0, t1 = piece
-            sums = banks.tile([P, 2, P], F32, name="bank")
+        def finish_on_tensor(nt, prods):
+            halves = [slice(0, T // 2), slice(T // 2, T)]
+            sums = [banks.tile([P, 2, P], F32, name="bank") for half in halves]
             for r in range(2):
-                turn_blocks(sums, prods[r], r == 0, r == 1)
-            turned = stage.tile([P, 2 * P], F32, name="turned", bufs=2)
-            nc.scalar.copy(out=turned[:], in_=sums[:].rearrange("p b n -> p (b n)"))
-            back = banks.tile([P, 2, P], F32, name="bank")
-            turn_blocks(back, turned, True, True)
-            res = stage.tile([P, 2 * P], F32, name="res", bufs=4)
-            nc.scalar.copy(out=res[:], in_=back[:].rearrange("p b n -> p (b n)"))
-            nc.sync.dma_start(out=out[nt * P : (nt + 1) * P, t0:t1], in_=res[:])
+                for half, bank in zip(halves, sums):
+                    turn_blocks(bank, prods[r][:, half], r == 0, r == 1)
+            turned = [stage.tile([P, 2 * P], F32, name="turned", bufs=2) for half in halves]
+            for half in range(2):
+                nc.scalar.copy(out=turned[half][:], in_=sums[half][:].rearrange("p b n -> p (b n)"))
+            for half in range(2):
+                back = banks.tile([P, 2, P], F32, name="bank")
+                turn_blocks(back, turned[half][:], True, True)
+                res = stage.tile([P, 2 * P], F32, name="res", bufs=4)
+                nc.scalar.copy(out=res[:], in_=back[:].rearrange("p b n -> p (b n)"))
+                nc.sync.dma_start(out=out[nt * P : (nt + 1) * P, halves[half]], in_=res[:])
 
-        for piece in ((0, 0, T // 2), (0, T // 2, T)):
-            finish_on_tensor(piece, [fetch(piece, 0), fetch(piece, 1)])
-        wide, narrow = (1, 0, T - LAST_PIECE), (1, T - LAST_PIECE, T)
-        prods = [fetch(wide, 0), fetch(wide, 1)]
-        first = fetch(narrow, 0)
-        finish(wide, prods)
-        finish(narrow, [first, fetch(narrow, 1)])
+        finish_on_tensor(0, [fetch(0, 0), fetch(0, 1)])
+        prods = [fetch(1, 0), fetch(1, 1)]
+        finish(1, 0, T - LAST_PIECE, prods)
+        finish(1, T - LAST_PIECE, T, prods)

@@ -36,8 +36,9 @@ PLACE_BYTES = 4 * PACK * H
 
 SCALAR_ALONE = 10
 T_HALF = PACK // 2
+VECTOR_ALONE = (13, 15)
 T_ORDER = (2, 3, 0, 1)
-GELU_AFTER = {7: 0, 11: 1, 16: 2}
+GELU_AFTER = {9: 0, 12: 1, 16: 2}
 LAST_W2_AT = 12
 LAST_SCALES_AT = 2
 POS_AT = 6
@@ -104,13 +105,19 @@ def tile_moe_pkd_mlp_gelu_kernel(tc, x_words, x_scales, w1, w2, gate, offs, pos1
                     b = o // PLANES
                     nc.vector.tensor_copy(out=slot_scales[g][:, b, :], in_=tok_scales[b][:].indirect(pair_list(g)))
 
-        def round_w1(grouped, raw, j0, shared):
+        def round_w1(grouped, raw, j0, copies):
             dst = grouped[:].rearrange("p t m j -> p m j t")[:, :, j0 : j0 + raw.shape[1], :]
             src = raw[:].rearrange("p j (m t) -> p m j t", t=PACK)
-            split = T_HALF if shared else PACK
-            nc.scalar.copy(out=dst[:, :, :, 0:split], in_=src[:, :, :, 0:split])
-            if shared:
-                nc.vector.tensor_copy(out=dst[:, :, :, split:PACK], in_=src[:, :, :, split:PACK])
+            share = PACK // len(copies)
+            for i, copy in enumerate(copies):
+                copy(out=dst[:, :, :, i * share : (i + 1) * share], in_=src[:, :, :, i * share : (i + 1) * share])
+
+        def rounders(n):
+            if n < SCALAR_ALONE:
+                return [nc.scalar.copy]
+            if n in VECTOR_ALONE:
+                return [nc.vector.tensor_copy, nc.vector.tensor_copy]
+            return [nc.scalar.copy, nc.vector.tensor_copy]
 
         def quantize(words, scales, c0, c1, values):
             nc.vector.quantize_mx(out=words[:, c0:c1].bitcast(FP8X4), scales=scales[:, c0:c1], in_=values)
@@ -146,7 +153,7 @@ def tile_moe_pkd_mlp_gelu_kernel(tc, x_words, x_scales, w1, w2, gate, offs, pos1
             return grouped
 
         def w2_tile(width):
-            return stage.tile([P, width, PACK], BF16, name="w2_grouped", align_bytes=64)
+            return stage.tile([P, width, PACK], BF16, name="w2_grouped", align_bytes=64, bufs=3)
 
         def quantize_w2(grouped):
             width = grouped.shape[1]
@@ -205,12 +212,12 @@ def tile_moe_pkd_mlp_gelu_kernel(tc, x_words, x_scales, w1, w2, gate, offs, pos1
                 if n > 0:
                     raw = load([P, PACK, H], w1_rows(n))
                 grouped = stage.tile([P, PACK, P, PACK], BF16, name="w1_grouped", align_bytes=64, bufs=9)
-                round_w1(grouped, raw, 0, n >= SCALAR_ALONE)
+                round_w1(grouped, raw, 0, rounders(n))
                 quantize(words, scales, 0, H, grouped[:].rearrange("p t m j -> p (t m j)"))
             else:
                 grouped = turn.tile([P, PACK, P, PACK], BF16, name="w1_last", tag="after_w1", align_bytes=64)
                 for j0 in (0, PACK // 2):
-                    round_w1(grouped, load([P, PACK // 2, H], w1_rows(n)[:, j0 : j0 + PACK // 2, :]), j0, True)
+                    round_w1(grouped, load([P, PACK // 2, H], w1_rows(n)[:, j0 : j0 + PACK // 2, :]), j0, rounders(n))
                 for t0 in (T_HALF, 0):
                     share = grouped[:, t0 : t0 + T_HALF].rearrange("p t m j -> p (t m j)")
                     quantize(words, scales, t0 * P, (t0 + T_HALF) * P, share)
@@ -265,14 +272,15 @@ def tile_moe_pkd_mlp_gelu_kernel(tc, x_words, x_scales, w1, w2, gate, offs, pos1
         make_y(turn_bank, 1, [(q2[1], 0, 2, 0, C), (last_q, P, last, 0, C)])
         make_y(banks, 1, [(q0[1], 0, 0, 0, C), (q1[1], 0, 1, 0, C)])
 
-        def fetch(nt, r):
-            prod = stage.tile([P, T], F32, name="prod", bufs=4)
-            nc.vector.tensor_tensor(prod[:], y_sb[nt][:].indirect(pos_sb[r][:]), gates[r][:], MULT)
+        def fetch(nt, r, t0, t1):
+            prod = stage.tile([P, t1 - t0], F32, name="prod", bufs=5)
+            entries = pos_sb[r][:, t0 // LIST_ROWS : t1 // LIST_ROWS]
+            nc.vector.tensor_tensor(prod[:], y_sb[nt][:].indirect(entries), gates[r][:, t0:t1], MULT)
             return prod
 
-        def finish(nt, t0, t1, prods):
+        def finish(nt, t0, t1, first, second):
             res = stage.tile([P, t1 - t0], F32, name="res", bufs=4)
-            nc.vector.tensor_tensor(res[:], prods[0][:, t0:t1], prods[1][:, t0:t1], ADD)
+            nc.vector.tensor_tensor(res[:], first, second, ADD)
             nc.sync.dma_start(out=out[nt * P : (nt + 1) * P, t0:t1], in_=res[:])
 
         def turn_blocks(bank, src, start, stop):
@@ -302,7 +310,7 @@ def tile_moe_pkd_mlp_gelu_kernel(tc, x_words, x_scales, w1, w2, gate, offs, pos1
                 nc.scalar.copy(out=res[:], in_=back[:].rearrange("p b n -> p (b n)"))
                 nc.sync.dma_start(out=out[nt * P : (nt + 1) * P, halves[half]], in_=res[:])
 
-        finish_on_tensor(0, [fetch(0, 0), fetch(0, 1)])
-        prods = [fetch(1, 0), fetch(1, 1)]
-        finish(1, 0, T - LAST_PIECE, prods)
-        finish(1, T - LAST_PIECE, T, prods)
+        finish_on_tensor(0, [fetch(0, 0, 0, T), fetch(0, 1, 0, T)])
+        first = fetch(1, 0, 0, T)
+        for t0, t1 in ((0, T - LAST_PIECE), (T - LAST_PIECE, T)):
+            finish(1, t0, t1, first[:, t0:t1], fetch(1, 1, t0, t1)[:])

@@ -273,7 +273,7 @@ def tile_moe_pkd_mlp_gelu_kernel(tc, x_words, x_scales, w1, w2, gate, offs, pos1
         make_y(banks, 1, [(q0[1], 0, 0, 0, C), (q1[1], 0, 1, 0, C)])
 
         def fetch(nt, r, t0, t1):
-            prod = stage.tile([P, t1 - t0], F32, name="prod", bufs=5)
+            prod = stage.tile([P, t1 - t0], F32, name="prod%d_%d_%d" % (nt, r, t0), bufs=1)
             entries = pos_sb[r][:, t0 // LIST_ROWS : t1 // LIST_ROWS]
             nc.vector.tensor_tensor(prod[:], y_sb[nt][:].indirect(entries), gates[r][:, t0:t1], MULT)
             return prod
@@ -294,12 +294,13 @@ def tile_moe_pkd_mlp_gelu_kernel(tc, x_words, x_scales, w1, w2, gate, offs, pos1
                     stop=stop and b == 1,
                 )
 
-        def finish_on_tensor(nt, prods):
+        def finish_on_tensor(nt, first, seconds):
             halves = [slice(0, T // 2), slice(T // 2, T)]
             sums = [banks.tile([P, 2, P], F32, name="bank") for half in halves]
-            for r in range(2):
-                for half, bank in zip(halves, sums):
-                    turn_blocks(bank, prods[r][:, half], r == 0, r == 1)
+            for half, bank in zip(halves, sums):
+                turn_blocks(bank, first[:, half], True, False)
+            for second, bank in zip(seconds, sums):
+                turn_blocks(bank, second[:], False, True)
             turned = [stage.tile([P, 2 * P], F32, name="turned", bufs=2) for half in halves]
             for half in range(2):
                 nc.scalar.copy(out=turned[half][:], in_=sums[half][:].rearrange("p b n -> p (b n)"))
@@ -310,7 +311,7 @@ def tile_moe_pkd_mlp_gelu_kernel(tc, x_words, x_scales, w1, w2, gate, offs, pos1
                 nc.scalar.copy(out=res[:], in_=back[:].rearrange("p b n -> p (b n)"))
                 nc.sync.dma_start(out=out[nt * P : (nt + 1) * P, halves[half]], in_=res[:])
 
-        finish_on_tensor(0, [fetch(0, 0, 0, T), fetch(0, 1, 0, T)])
+        finish_on_tensor(0, fetch(0, 0, 0, T), [fetch(0, 1, 0, T // 2), fetch(0, 1, T // 2, T)])
         first = fetch(1, 0, 0, T)
         for t0, t1 in ((0, T - LAST_PIECE), (T - LAST_PIECE, T)):
             finish(1, t0, t1, first[:, t0:t1], fetch(1, 1, t0, t1)[:])

@@ -42,7 +42,7 @@ GELU_AFTER = {9: 0, 12: 1, 16: 2}
 LAST_W2_AT = 12
 LAST_SCALES_AT = 2
 POS_AT = 6
-LAST_PIECE = 128
+LAST_PIECE = 256
 
 
 def tile_moe_pkd_mlp_gelu_kernel(tc, x_words, x_scales, w1, w2, gate, offs, pos1, pos2, out):
@@ -313,5 +313,7 @@ def tile_moe_pkd_mlp_gelu_kernel(tc, x_words, x_scales, w1, w2, gate, offs, pos1
 
         finish_on_tensor(0, fetch(0, 0, 0, T), [fetch(0, 1, 0, T // 2), fetch(0, 1, T // 2, T)])
         first = fetch(1, 0, 0, T)
-        for t0, t1 in ((0, T - LAST_PIECE), (T - LAST_PIECE, T)):
-            finish(1, t0, t1, first[:, t0:t1], fetch(1, 1, t0, t1)[:])
+        pieces = ((0, T - LAST_PIECE), (T - LAST_PIECE, T))
+        seconds = [fetch(1, 1, t0, t1) for t0, t1 in pieces]
+        for (t0, t1), second in zip(pieces, seconds):
+            finish(1, t0, t1, first[:, t0:t1], second[:])

@@ -14,6 +14,7 @@ U16 = mybir.dt.uint16
 U8 = mybir.dt.uint8
 FP8X4 = mybir.dt.float8_e4m3fn_x4
 GELU = mybir.ActivationFunctionType.Gelu_apprx_tanh
+COPY = mybir.ActivationFunctionType.Copy
 MULT = mybir.AluOpType.mult
 ADD = mybir.AluOpType.add
 
@@ -42,7 +43,7 @@ GELU_AFTER = {9: 0, 12: 1, 16: 2}
 LAST_W2_AT = 12
 LAST_SCALES_AT = 2
 POS_AT = 6
-LAST_PIECE = 256
+GATE_ROWS_AT = 8
 
 
 def tile_moe_pkd_mlp_gelu_kernel(tc, x_words, x_scales, w1, w2, gate, offs, pos1, pos2, out):
@@ -153,7 +154,7 @@ def tile_moe_pkd_mlp_gelu_kernel(tc, x_words, x_scales, w1, w2, gate, offs, pos1
             return grouped
 
         def w2_tile(width):
-            return stage.tile([P, width, PACK], BF16, name="w2_grouped", align_bytes=64, bufs=3)
+            return stage.tile([P, width, PACK], BF16, name="w2_grouped", align_bytes=64, bufs=1)
 
         def quantize_w2(grouped):
             width = grouped.shape[1]
@@ -185,6 +186,9 @@ def tile_moe_pkd_mlp_gelu_kernel(tc, x_words, x_scales, w1, w2, gate, offs, pos1
             nc.vector.memset(tok_words[o][:, T:], 0)
         identity = keep.tile([P, P], F32, name="identity")
         make_identity(nc, identity[:])
+        gate_rows = keep.tile([P, P], F32, name="gate_rows")
+        nc.gpsimd.memset(gate_rows[:], 0.0)
+        gate_cols = keep.tile([P, 4], F32, name="gate_cols")
         nc.sync.dma_start(offs_sb[:], offs)
 
         last = E - 1
@@ -203,6 +207,11 @@ def tile_moe_pkd_mlp_gelu_kernel(tc, x_words, x_scales, w1, w2, gate, offs, pos1
             if n == POS_AT:
                 nc.sync.dma_start(pos_sb[0][:], pos1)
                 nc.sync.dma_start(pos_sb[1][:], pos2)
+            if n == GATE_ROWS_AT:
+                nc.sync.dma_start(out=gate_rows[0:4, :], in_=gate[:, 0, 0 : 2 * P].rearrange("r (b c) -> r b c", c=P))
+                gate_bank = turn_bank.tile([P, P], F32, name="bank")
+                nc.tensor.transpose(gate_bank[:], gate_rows[:], identity[:])
+                nc.scalar.copy(out=gate_cols[:], in_=gate_bank[:, 0:4])
             if n == LAST_W2_AT:
                 last_rounded = round_w2(nc.vector.tensor_copy, w2_tile(N), load_w2(last, 0, N), 0)
 
@@ -236,41 +245,37 @@ def tile_moe_pkd_mlp_gelu_kernel(tc, x_words, x_scales, w1, w2, gate, offs, pos1
 
         raw2 = load_w2(2, 0, N)
         raw1 = load_w2(1, 0, N)
-        raw0 = [load_w2(0, nt * P, (nt + 1) * P) for nt in range(N_TILES)]
+        raw0 = load_w2(0, 0, N)
         gates = [load([P, T], gate[r, 0:P, :]) for r in range(2)]
 
-        def in_turn(tag):
-            return turn.tile([P, P, PACK], BF16, name="w2_" + tag, tag=tag, align_bytes=64)
+        def late_tile(e, nt):
+            return stage.tile([P, P, PACK], BF16, name="w2_late%d_%d" % (e, nt), align_bytes=64, bufs=1)
 
-        rounded2 = [
-            round_w2(nc.scalar.copy, w2_tile(P), raw2, 0),
-            round_w2(nc.vector.tensor_copy, in_turn("after_w1"), raw2, P),
-        ]
-        h_halves = [
-            stage.tile([P, HALF, PACK], BF16, name="h_first", align_bytes=64, bufs=1),
-            turn.tile([P, HALF, PACK], BF16, name="h_second", tag="after_h", align_bytes=64),
-        ]
+        def round_late(copy, e, raw, nt):
+            return round_w2(copy, late_tile(e, nt), raw, nt * P)
+
+        rounded2 = [round_late(nc.scalar.copy, 2, raw2, 0), round_late(nc.vector.tensor_copy, 2, raw2, 1)]
+        h_halves = [stage.tile([P, HALF, PACK], BF16, name="h_last%d" % half, align_bytes=64, bufs=1) for half in range(2)]
         for half in range(2):
             gelu(h_halves[half][:], pairs[last][half])
-        q2 = [quantize_w2(rounded2[0])]
-        rounded1 = round_w2(nc.vector.tensor_copy, w2_tile(P), raw1, 0)
-        q2.append(quantize_w2(rounded2[1]))
-        q1 = [quantize_w2(rounded1)]
+        q2b = quantize_w2(rounded2[1])
+        q2a = quantize_w2(rounded2[0])
+        rounded1a = round_late(nc.vector.tensor_copy, 1, raw1, 0)
         quantize_h(last, 0, HALF, h_halves[0])
-        rounded0 = round_w2(nc.vector.tensor_copy, in_turn("after_w1"), raw0[0], 0)
+        q1a = quantize_w2(rounded1a)
+        rounded1b = round_late(nc.vector.tensor_copy, 1, raw1, 1)
+        rounded0a = round_late(nc.vector.tensor_copy, 0, raw0, 0)
         quantize_h(last, HALF, C, h_halves[1])
-        q0 = [quantize_w2(rounded0)]
-        both = turn.tile([P, N, PACK], BF16, name="w2_both", tag="after_h", align_bytes=64)
-        round_w2(nc.vector.tensor_copy, both[:, 0:P], raw1, P)
-        round_w2(nc.vector.tensor_copy, both[:, P:N], raw0[1], 0)
-        q1.append(quantize_w2(both[:, 0:P]))
-        q0.append(quantize_w2(both[:, P:N]))
-        make_y(banks, 0, [(q1[0], 0, 1, 0, C), (q2[0], 0, 2, 0, C)])
-        make_y(banks, 0, [(last_q, 0, last, 0, HALF)])
-        make_y(banks, 0, [(last_q, 0, last, HALF, C)])
-        make_y(turn_bank, 0, [(q0[0], 0, 0, 0, C)])
-        make_y(turn_bank, 1, [(q2[1], 0, 2, 0, C), (last_q, P, last, 0, C)])
-        make_y(banks, 1, [(q0[1], 0, 0, 0, C), (q1[1], 0, 1, 0, C)])
+        q0a = quantize_w2(rounded0a)
+        q1b = quantize_w2(rounded1b)
+        q0b = quantize_w2(round_late(nc.vector.tensor_copy, 0, raw0, 1))
+        make_y(banks, 0, [(q2a, 0, 2, 0, C)])
+        make_y(banks, 1, [(q2b, 0, 2, 0, C)])
+        make_y(banks, 0, [(q1a, 0, 1, 0, C)])
+        make_y(banks, 0, [(last_q, 0, last, 0, C)])
+        make_y(banks, 1, [(last_q, P, last, 0, C)])
+        make_y(banks, 0, [(q0a, 0, 0, 0, C)])
+        make_y(banks, 1, [(q0b, 0, 0, 0, C), (q1b, 0, 1, 0, C)])
 
         def fetch(nt, r, t0, t1):
             prod = stage.tile([P, t1 - t0], F32, name="prod%d_%d_%d" % (nt, r, t0), bufs=1)
@@ -294,26 +299,34 @@ def tile_moe_pkd_mlp_gelu_kernel(tc, x_words, x_scales, w1, w2, gate, offs, pos1
                     stop=stop and b == 1,
                 )
 
-        def finish_on_tensor(nt, first, seconds):
-            halves = [slice(0, T // 2), slice(T // 2, T)]
-            sums = [banks.tile([P, 2, P], F32, name="bank") for half in halves]
-            for half, bank in zip(halves, sums):
-                turn_blocks(bank, first[:, half], True, False)
-            for second, bank in zip(seconds, sums):
-                turn_blocks(bank, second[:], False, True)
-            turned = [stage.tile([P, 2 * P], F32, name="turned", bufs=2) for half in halves]
-            for half in range(2):
-                nc.scalar.copy(out=turned[half][:], in_=sums[half][:].rearrange("p b n -> p (b n)"))
-            for half in range(2):
-                back = banks.tile([P, 2, P], F32, name="bank")
-                turn_blocks(back, turned[half][:], True, True)
-                res = stage.tile([P, 2 * P], F32, name="res", bufs=4)
-                nc.scalar.copy(out=res[:], in_=back[:].rearrange("p b n -> p (b n)"))
-                nc.sync.dma_start(out=out[nt * P : (nt + 1) * P, halves[half]], in_=res[:])
+        def turn_back(nt, t0, parts):
+            back = banks.tile([P, 2, P], F32, name="bank")
+            for i, part in enumerate(parts):
+                turn_blocks(back, part[:], i == 0, i == len(parts) - 1)
+            res = stage.tile([P, 2 * P], F32, name="res", bufs=4)
+            nc.scalar.copy(out=res[:], in_=back[:].rearrange("p b n -> p (b n)"))
+            nc.scalar.dma_start(out=out[nt * P : (nt + 1) * P, t0 : t0 + 2 * P], in_=res[:])
 
-        finish_on_tensor(0, fetch(0, 0, 0, T), [fetch(0, 1, 0, T // 2), fetch(0, 1, T // 2, T)])
+        mid = T // 2
+        products = [fetch(0, r, mid, T) for r in range(2)]
         first = fetch(1, 0, 0, T)
-        pieces = ((0, T - LAST_PIECE), (T - LAST_PIECE, T))
-        seconds = [fetch(1, 1, t0, t1) for t0, t1 in pieces]
-        for (t0, t1), second in zip(pieces, seconds):
-            finish(1, t0, t1, first[:, t0:t1], second[:])
+        seconds = [fetch(1, 1, t0, t0 + mid) for t0 in (0, mid)]
+
+        picked = [stage.tile([P, mid], F32, name="picked%d" % r, bufs=1) for r in range(2)]
+        for r in range(2):
+            nc.scalar.activation(picked[r][:], y_sb[0][:].indirect(pos_sb[r][:, 0 : mid // LIST_ROWS]), COPY)
+        total = banks.tile([P, 2, P], F32, name="bank")
+        for r in range(2):
+            turn_blocks(total, products[r][:], r == 0, r == 1)
+        turned = [stage.tile([P, mid], F32, name="turned", bufs=3) for part in range(3)]
+        nc.scalar.copy(out=turned[2][:], in_=total[:].rearrange("p b n -> p (b n)"))
+        for r in range(2):
+            bank = banks.tile([P, 2, P], F32, name="bank")
+            turn_blocks(bank, picked[r][:], True, True)
+            for b in range(2):
+                column = gate_cols[:, 2 * r + b : 2 * r + b + 1]
+                nc.scalar.activation(turned[r][:, b * P : (b + 1) * P], bank[:, b, :], COPY, scale=column)
+        turn_back(0, mid, turned[2:])
+        turn_back(0, 0, turned[:2])
+        for t0, second in zip((0, mid), seconds):
+            finish(1, t0, t0 + mid, first[:, t0 : t0 + mid], second[:])

@@ -106,8 +106,8 @@ def tile_moe_pkd_mlp_gelu_kernel(tc, x_words, x_scales, w1, w2, gate, offs, pos1
                     b = o // PLANES
                     nc.vector.tensor_copy(out=slot_scales[g][:, b, :], in_=tok_scales[b][:].indirect(pair_list(g)))
 
-        def round_w1(grouped, raw, j0, copies):
-            dst = grouped[:].rearrange("p t m j -> p m j t")[:, :, j0 : j0 + raw.shape[1], :]
+        def round_w1(grouped, raw, copies):
+            dst = grouped.rearrange("p t m j -> p m j t")
             src = raw[:].rearrange("p j (m t) -> p m j t", t=PACK)
             share = PACK // len(copies)
             for i, copy in enumerate(copies):
@@ -221,15 +221,16 @@ def tile_moe_pkd_mlp_gelu_kernel(tc, x_words, x_scales, w1, w2, gate, offs, pos1
                 if n > 0:
                     raw = load([P, PACK, H], w1_rows(n))
                 grouped = stage.tile([P, PACK, P, PACK], BF16, name="w1_grouped", align_bytes=64, bufs=9)
-                round_w1(grouped, raw, 0, rounders(n))
+                round_w1(grouped[:], raw, rounders(n))
                 quantize(words, scales, 0, H, grouped[:].rearrange("p t m j -> p (t m j)"))
             else:
                 grouped = turn.tile([P, PACK, P, PACK], BF16, name="w1_last", tag="after_w1", align_bytes=64)
-                for j0 in (0, PACK // 2):
-                    round_w1(grouped, load([P, PACK // 2, H], w1_rows(n)[:, j0 : j0 + PACK // 2, :]), j0, rounders(n))
-                for t0 in (T_HALF, 0):
-                    share = grouped[:, t0 : t0 + T_HALF].rearrange("p t m j -> p (t m j)")
-                    quantize(words, scales, t0 * P, (t0 + T_HALF) * P, share)
+                for m0 in (0, P // 2):
+                    raw = load([P, PACK, H // 2], w1_rows(n)[:, :, PACK * m0 : PACK * m0 + H // 2])
+                    round_w1(grouped[:, :, m0 : m0 + P // 2], raw, rounders(n))
+                    for t in T_ORDER:
+                        values = grouped[:, t, m0 : m0 + P // 2].rearrange("p m j -> p (m j)")
+                        quantize(words, scales, t * P + m0, t * P + m0 + P // 2, values)
 
             if n - 1 in GELU_AFTER:
                 quantize_h(GELU_AFTER[n - 1], 0, C, h)

@@ -244,39 +244,37 @@ def tile_moe_pkd_mlp_gelu_kernel(tc, x_words, x_scales, w1, w2, gate, offs, pos1
                 pairs.append([banks.tile([P, PACK, HALF], F32, name="bank") for half in range(2)])
             layer1_pass(pairs[e], n, words, scales)
 
-        raw2 = load_w2(2, 0, N)
-        raw1 = load_w2(1, 0, N)
-        raw0 = load_w2(0, 0, N)
+        late = [(e, nt) for nt in range(N_TILES) for e in (2, 1, 0)]
+        raws = {(e, nt): load_w2(e, nt * P, (nt + 1) * P) for e, nt in late}
         gates = [load([P, T], gate[r, 0:P, :]) for r in range(2)]
 
-        def late_tile(e, nt):
-            return stage.tile([P, P, PACK], BF16, name="w2_late%d_%d" % (e, nt), align_bytes=64, bufs=1)
+        def round_late(copy, e, nt):
+            grouped = stage.tile([P, P, PACK], BF16, name="w2_late%d_%d" % (e, nt), align_bytes=64, bufs=1)
+            return round_w2(copy, grouped, raws[e, nt], 0)
 
-        def round_late(copy, e, raw, nt):
-            return round_w2(copy, late_tile(e, nt), raw, nt * P)
-
-        rounded2 = [round_late(nc.scalar.copy, 2, raw2, 0), round_late(nc.vector.tensor_copy, 2, raw2, 1)]
+        rounded2a = round_late(nc.vector.tensor_copy, 2, 0)
+        rounded1a = round_late(nc.scalar.copy, 1, 0)
         h_halves = [stage.tile([P, HALF, PACK], BF16, name="h_last%d" % half, align_bytes=64, bufs=1) for half in range(2)]
         for half in range(2):
             gelu(h_halves[half][:], pairs[last][half])
-        q2b = quantize_w2(rounded2[1])
-        q2a = quantize_w2(rounded2[0])
-        rounded1a = round_late(nc.vector.tensor_copy, 1, raw1, 0)
-        quantize_h(last, 0, HALF, h_halves[0])
+        q2a = quantize_w2(rounded2a)
+        rounded0a = round_late(nc.vector.tensor_copy, 0, 0)
         q1a = quantize_w2(rounded1a)
-        rounded1b = round_late(nc.vector.tensor_copy, 1, raw1, 1)
-        rounded0a = round_late(nc.vector.tensor_copy, 0, raw0, 0)
-        quantize_h(last, HALF, C, h_halves[1])
+        rounded2b = round_late(nc.vector.tensor_copy, 2, 1)
+        quantize_h(last, 0, HALF, h_halves[0])
         q0a = quantize_w2(rounded0a)
+        rounded1b = round_late(nc.vector.tensor_copy, 1, 1)
+        quantize_h(last, HALF, C, h_halves[1])
+        q2b = quantize_w2(rounded2b)
+        rounded0b = round_late(nc.vector.tensor_copy, 0, 1)
         q1b = quantize_w2(rounded1b)
-        q0b = quantize_w2(round_late(nc.vector.tensor_copy, 0, raw0, 1))
-        make_y(banks, 0, [(q2a, 0, 2, 0, C)])
-        make_y(banks, 1, [(q2b, 0, 2, 0, C)])
-        make_y(banks, 0, [(q1a, 0, 1, 0, C)])
-        make_y(banks, 0, [(last_q, 0, last, 0, C)])
-        make_y(banks, 1, [(last_q, P, last, 0, C)])
-        make_y(banks, 0, [(q0a, 0, 0, 0, C)])
-        make_y(banks, 1, [(q0b, 0, 0, 0, C), (q1b, 0, 1, 0, C)])
+        q0b = quantize_w2(rounded0b)
+        make_y(banks, 0, [(q0a, 0, 0, 0, C), (q1a, 0, 1, 0, C)])
+        make_y(banks, 0, [(q2a, 0, 2, 0, C), (last_q, 0, last, 0, HALF)])
+        make_y(banks, 0, [(last_q, 0, last, HALF, C)])
+        make_y(banks, 1, [(q2b, 0, 2, 0, C), (last_q, P, last, 0, C)])
+        make_y(banks, 1, [(q1b, 0, 1, 0, C)])
+        make_y(banks, 1, [(q0b, 0, 0, 0, C)])
 
         def fetch(nt, r, t0, t1):
             prod = stage.tile([P, t1 - t0], F32, name="prod%d_%d_%d" % (nt, r, t0), bufs=1)

@@ -35,11 +35,10 @@ LIST_ROWS = 16
 RING = 10
 PLACE_BYTES = 4 * PACK * H
 
-SCALAR_ALONE = 10
+SCALAR_ALONE = 7
 T_HALF = PACK // 2
-VECTOR_ALONE = (13, 15)
 T_ORDER = (2, 3, 0, 1)
-GELU_AFTER = {9: 0, 12: 1, 16: 2}
+GELU_AFTER = {9: 0, 13: 1, 16: 2}
 LAST_W2_AT = 12
 LAST_SCALES_AT = 2
 POS_AT = 6
@@ -116,8 +115,6 @@ def tile_moe_pkd_mlp_gelu_kernel(tc, x_words, x_scales, w1, w2, gate, offs, pos1
         def rounders(n):
             if n < SCALAR_ALONE:
                 return [nc.scalar.copy]
-            if n in VECTOR_ALONE:
-                return [nc.vector.tensor_copy, nc.vector.tensor_copy]
             return [nc.scalar.copy, nc.vector.tensor_copy]
 
         def quantize(words, scales, c0, c1, values):

@@ -66,26 +66,26 @@ def tile_moe_pkd_mlp_gelu_kernel(tc, x_words, x_scales, w1, w2, gate, offs, pos1
         h_scales = [keep.tile([P, C], U8, name="h_scales%d" % e, align_bytes=64) for e in range(E)]
         y_sb = [keep.tile([P, SLOTS], F32, name="y_sb%d" % nt) for nt in range(N_TILES)]
 
-        places = list(range(RING))
         filled = []
 
         def on_place(place, shape, dtype, name, skip):
             return ring.tile(shape, dtype, name=name, align_bytes=64, offset=place * PLACE_BYTES + skip)
 
-        def load(shape, src):
-            place = places.pop(0)
-            places.append(place)
+        def load(shape, src, place, skip=0):
             filled.append(place)
-            raw = on_place(place, shape, F32, "raw%d" % len(filled), 0)
+            raw = on_place(place, shape, F32, "raw%d" % len(filled), skip)
             nc.sync.dma_start(out=raw[:], in_=src)
             return raw
+
+        def place_of(n):
+            return n if n < RING else (n - RING) ^ 1
 
         def w1_rows(n):
             e, o = divmod(n, PASSES)
             return w1[e, o * K_PASS : (o + 1) * K_PASS, :].rearrange("(p j) i -> p j i", j=PACK)
 
-        def load_w2(e, n0, n1):
-            return load([P, PACK, n1 - n0], w2[e, :, n0:n1].rearrange("(p j) n -> p j n", j=PACK))
+        def load_w2(e, n0, n1, place, skip):
+            return load([P, PACK, n1 - n0], w2[e, :, n0:n1].rearrange("(p j) n -> p j n", j=PACK), place, skip)
 
         def load_scale_rows(b):
             o0, o1 = b * PLANES, min((b + 1) * PLANES, PASSES)
@@ -195,7 +195,7 @@ def tile_moe_pkd_mlp_gelu_kernel(tc, x_words, x_scales, w1, w2, gate, offs, pos1
             if e == 0:
                 nc.sync.dma_start(out=tok_words[o][:, 0:T], in_=x_words[o].rearrange("p t r -> p (t r)").bitcast(I32))
             if n == 0:
-                raw = load([P, PACK, H], w1_rows(n))
+                raw = load([P, PACK, H], w1_rows(n), place_of(n))
                 load_scale_rows(0)
             if n == LAST_SCALES_AT:
                 load_scale_rows(1)
@@ -210,20 +210,20 @@ def tile_moe_pkd_mlp_gelu_kernel(tc, x_words, x_scales, w1, w2, gate, offs, pos1
                 nc.tensor.transpose(gate_bank[:], gate_rows[:], identity[:])
                 nc.scalar.copy(out=gate_cols[:], in_=gate_bank[:, 0:4])
             if n == LAST_W2_AT:
-                last_rounded = round_w2(nc.vector.tensor_copy, w2_tile(N), load_w2(last, 0, N), 0)
+                last_rounded = round_w2(nc.vector.tensor_copy, w2_tile(N), load_w2(last, 0, N, RING, 0), 0)
 
             words = codes.tile([P, H], U32, name="w1_codes", align_bytes=64)
             scales = codes.tile([P, H], U8, name="w1_scales", align_bytes=64)
             if n < CHUNKS - 1:
                 if n > 0:
-                    raw = load([P, PACK, H], w1_rows(n))
+                    raw = load([P, PACK, H], w1_rows(n), place_of(n))
                 grouped = stage.tile([P, PACK, P, PACK], BF16, name="w1_grouped", align_bytes=64, bufs=9)
                 round_w1(grouped[:], raw, rounders(n))
                 quantize(words, scales, 0, H, grouped[:].rearrange("p t m j -> p (t m j)"))
             else:
                 grouped = turn.tile([P, PACK, P, PACK], BF16, name="w1_last", tag="after_w1", align_bytes=64)
                 for m0 in (0, P // 2):
-                    raw = load([P, PACK, H // 2], w1_rows(n)[:, :, PACK * m0 : PACK * m0 + H // 2])
+                    raw = load([P, PACK, H // 2], w1_rows(n)[:, :, PACK * m0 : PACK * m0 + H // 2], place_of(n), m0 * 64)
                     round_w1(grouped[:, :, m0 : m0 + P // 2], raw, rounders(n))
                     for t in T_ORDER:
                         values = grouped[:, t, m0 : m0 + P // 2].rearrange("p m j -> p (m j)")
@@ -242,8 +242,8 @@ def tile_moe_pkd_mlp_gelu_kernel(tc, x_words, x_scales, w1, w2, gate, offs, pos1
             layer1_pass(pairs[e], n, words, scales)
 
         late = [(e, nt) for nt in range(N_TILES) for e in (2, 1, 0)]
-        raws = {(e, nt): load_w2(e, nt * P, (nt + 1) * P) for e, nt in late}
-        gates = [load([P, T], gate[r, 0:P, :]) for r in range(2)]
+        raws = {(e, nt): load_w2(e, nt * P, (nt + 1) * P, place_of(11 - i // 4), i % 4 * 2048) for i, (e, nt) in enumerate(late)}
+        gates = [load([P, T], gate[r, 0:P, :], place_of(10), (2 + r) * 2048) for r in range(2)]
 
         def round_late(copy, e, nt):
             grouped = stage.tile([P, P, PACK], BF16, name="w2_late%d_%d" % (e, nt), align_bytes=64, bufs=1)

@@ -36,6 +36,7 @@ RING = 10
 PLACE_BYTES = 4 * PACK * H
 
 SCALAR_ALONE = 7
+VECTOR_ALONE = (10, 14, 15)
 T_HALF = PACK // 2
 T_ORDER = (2, 3, 0, 1)
 GELU_AFTER = {9: 0, 13: 1, 16: 2}
@@ -113,8 +114,10 @@ def tile_moe_pkd_mlp_gelu_kernel(tc, x_words, x_scales, w1, w2, gate, offs, pos1
                 copy(out=dst[:, :, :, i * share : (i + 1) * share], in_=src[:, :, :, i * share : (i + 1) * share])
 
         def rounders(n):
-            if n < SCALAR_ALONE:
+            if n < SCALAR_ALONE or n == LAST_W2_AT:
                 return [nc.scalar.copy]
+            if n in VECTOR_ALONE:
+                return [nc.vector.tensor_copy]
             return [nc.scalar.copy, nc.vector.tensor_copy]
 
         def quantize(words, scales, c0, c1, values):
@@ -208,7 +211,7 @@ def tile_moe_pkd_mlp_gelu_kernel(tc, x_words, x_scales, w1, w2, gate, offs, pos1
                 nc.sync.dma_start(out=gate_rows[0:4, :], in_=gate[:, 0, 0 : 2 * P].rearrange("r (b c) -> r b c", c=P))
                 gate_bank = turn_bank.tile([P, P], F32, name="bank")
                 nc.tensor.transpose(gate_bank[:], gate_rows[:], identity[:])
-                nc.scalar.copy(out=gate_cols[:], in_=gate_bank[:, 0:4])
+                nc.vector.tensor_copy(out=gate_cols[:], in_=gate_bank[:, 0:4])
             if n == LAST_W2_AT:
                 last_rounded = round_w2(nc.vector.tensor_copy, w2_tile(N), load_w2(last, 0, N, RING, 0), 0)
 

@@ -36,14 +36,15 @@ RING = 10
 PLACE_BYTES = 4 * PACK * H
 
 SCALAR_ALONE = 7
-VECTOR_ALONE = (10, 14, 15)
+VECTOR_ALONE = (14, 15)
 T_HALF = PACK // 2
 T_ORDER = (2, 3, 0, 1)
 GELU_AFTER = {9: 0, 13: 1, 16: 2}
 LAST_W2_AT = 12
 LAST_SCALES_AT = 2
-POS_AT = 6
 GATE_ROWS_AT = 8
+LISTS_AFTER = 5
+GATE_SPREAD_AT = 13
 
 
 def tile_moe_pkd_mlp_gelu_kernel(tc, x_words, x_scales, w1, w2, gate, offs, pos1, pos2, out):
@@ -188,7 +189,8 @@ def tile_moe_pkd_mlp_gelu_kernel(tc, x_words, x_scales, w1, w2, gate, offs, pos1
         make_identity(nc, identity[:])
         gate_rows = keep.tile([P, P], F32, name="gate_rows")
         nc.gpsimd.memset(gate_rows[:], 0.0)
-        gate_cols = keep.tile([P, 4], F32, name="gate_cols")
+        gate_cols = keep.tile([P, 2 * T // P], F32, name="gate_cols")
+        gates = [keep.tile([P, T], F32, name="gate_sb%d" % r) for r in range(2)]
         nc.sync.dma_start(offs_sb[:], offs)
 
         last = E - 1
@@ -204,14 +206,18 @@ def tile_moe_pkd_mlp_gelu_kernel(tc, x_words, x_scales, w1, w2, gate, offs, pos1
                 load_scale_rows(1)
             if e == 0:
                 gather_tokens(o)
-            if n == POS_AT:
-                nc.sync.dma_start(pos_sb[0][:], pos1)
-                nc.sync.dma_start(pos_sb[1][:], pos2)
             if n == GATE_ROWS_AT:
-                nc.sync.dma_start(out=gate_rows[0:4, :], in_=gate[:, 0, 0 : 2 * P].rearrange("r (b c) -> r b c", c=P))
+                nc.sync.dma_start(out=gate_rows[0 : 2 * T // P, :], in_=gate[:, 0, :].rearrange("r (b c) -> r b c", c=P))
                 gate_bank = turn_bank.tile([P, P], F32, name="bank")
                 nc.tensor.transpose(gate_bank[:], gate_rows[:], identity[:])
-                nc.vector.tensor_copy(out=gate_cols[:], in_=gate_bank[:, 0:4])
+                nc.vector.tensor_copy(out=gate_cols[:], in_=gate_bank[:, 0 : 2 * T // P])
+            if n == GATE_SPREAD_AT:
+                for r in range(2):
+                    spread = banks.tile([P, T // P, P], F32, name="bank")
+                    for b in range(T // P):
+                        column = gate_cols[:, r * T // P + b : r * T // P + b + 1]
+                        nc.tensor.transpose(spread[:, b, :], column.to_broadcast([P, P]), identity[:])
+                    nc.vector.tensor_copy(out=gates[r][:], in_=spread[:].rearrange("p b c -> p (b c)"))
             if n == LAST_W2_AT:
                 last_rounded = round_w2(nc.vector.tensor_copy, w2_tile(N), load_w2(last, 0, N, RING, 0), 0)
 
@@ -220,7 +226,7 @@ def tile_moe_pkd_mlp_gelu_kernel(tc, x_words, x_scales, w1, w2, gate, offs, pos1
             if n < CHUNKS - 1:
                 if n > 0:
                     raw = load([P, PACK, H], w1_rows(n), place_of(n))
-                grouped = stage.tile([P, PACK, P, PACK], BF16, name="w1_grouped", align_bytes=64, bufs=9)
+                grouped = stage.tile([P, PACK, P, PACK], BF16, name="w1_grouped", align_bytes=64, bufs=8)
                 round_w1(grouped[:], raw, rounders(n))
                 quantize(words, scales, 0, H, grouped[:].rearrange("p t m j -> p (t m j)"))
             else:
@@ -245,8 +251,12 @@ def tile_moe_pkd_mlp_gelu_kernel(tc, x_words, x_scales, w1, w2, gate, offs, pos1
             layer1_pass(pairs[e], n, words, scales)
 
         late = [(e, nt) for nt in range(N_TILES) for e in (2, 1, 0)]
-        raws = {(e, nt): load_w2(e, nt * P, (nt + 1) * P, place_of(11 - i // 4), i % 4 * 2048) for i, (e, nt) in enumerate(late)}
-        gates = [load([P, T], gate[r, 0:P, :], place_of(10), (2 + r) * 2048) for r in range(2)]
+        raws = {}
+        for i, (e, nt) in enumerate(late):
+            raws[e, nt] = load_w2(e, nt * P, (nt + 1) * P, place_of(11 - i // 4), i % 4 * 2048)
+            if i == LISTS_AFTER:
+                nc.sync.dma_start(pos_sb[0][:], pos1)
+                nc.sync.dma_start(pos_sb[1][:], pos2)
 
         def round_late(copy, e, nt):
             grouped = stage.tile([P, P, PACK], BF16, name="w2_late%d_%d" % (e, nt), align_bytes=64, bufs=1)
@@ -323,7 +333,7 @@ def tile_moe_pkd_mlp_gelu_kernel(tc, x_words, x_scales, w1, w2, gate, offs, pos1
             bank = banks.tile([P, 2, P], F32, name="bank")
             turn_blocks(bank, picked[r][:], True, True)
             for b in range(2):
-                column = gate_cols[:, 2 * r + b : 2 * r + b + 1]
+                column = gate_cols[:, r * T // P + b : r * T // P + b + 1]
                 nc.scalar.activation(turned[r][:, b * P : (b + 1) * P], bank[:, b, :], COPY, scale=column)
         turn_back(0, mid, turned[2:])
         turn_back(0, 0, turned[:2])

@@ -36,15 +36,16 @@ RING = 10
 PLACE_BYTES = 4 * PACK * H
 
 SCALAR_ALONE = 7
-VECTOR_ALONE = (14, 15)
+VECTOR_ALONE = (7, 10, 14, 15)
+SCALAR_TOO = (8, 11, 12)
 T_HALF = PACK // 2
 T_ORDER = (2, 3, 0, 1)
-GELU_AFTER = {9: 0, 13: 1, 16: 2}
+GELU_AFTER = {9: 0, 13: 1, 15: 2}
 LAST_W2_AT = 12
 LAST_SCALES_AT = 2
 GATE_ROWS_AT = 8
 LISTS_AFTER = 5
-GATE_SPREAD_AT = 13
+GATE_SPREAD_AT = 14
 
 
 def tile_moe_pkd_mlp_gelu_kernel(tc, x_words, x_scales, w1, w2, gate, offs, pos1, pos2, out):
@@ -55,7 +56,8 @@ def tile_moe_pkd_mlp_gelu_kernel(tc, x_words, x_scales, w1, w2, gate, offs, pos1
         stage = ctx.enter_context(tc.tile_pool(name="stage", bufs=4))
         codes = ctx.enter_context(tc.tile_pool(name="codes", bufs=2 * PASSES))
         turn = ctx.enter_context(tc.tile_pool(name="turn", bufs=1))
-        banks = ctx.enter_context(tc.psum_pool(name="banks", bufs=7))
+        sums = ctx.enter_context(tc.psum_pool(name="sums", bufs=4))
+        banks = ctx.enter_context(tc.psum_pool(name="banks", bufs=3))
         turn_bank = ctx.enter_context(tc.psum_pool(name="turn_bank", bufs=1))
 
         offs_sb = keep.tile([P, SLOTS // LIST_ROWS], U16, name="offs_sb")
@@ -115,7 +117,7 @@ def tile_moe_pkd_mlp_gelu_kernel(tc, x_words, x_scales, w1, w2, gate, offs, pos1
                 copy(out=dst[:, :, :, i * share : (i + 1) * share], in_=src[:, :, :, i * share : (i + 1) * share])
 
         def rounders(n):
-            if n < SCALAR_ALONE or n == LAST_W2_AT:
+            if n < SCALAR_ALONE or n in SCALAR_TOO:
                 return [nc.scalar.copy]
             if n in VECTOR_ALONE:
                 return [nc.vector.tensor_copy]
@@ -213,11 +215,11 @@ def tile_moe_pkd_mlp_gelu_kernel(tc, x_words, x_scales, w1, w2, gate, offs, pos1
                 nc.vector.tensor_copy(out=gate_cols[:], in_=gate_bank[:, 0 : 2 * T // P])
             if n == GATE_SPREAD_AT:
                 for r in range(2):
-                    spread = banks.tile([P, T // P, P], F32, name="bank")
+                    spread = sums.tile([P, T // P, P], F32, name="bank")
                     for b in range(T // P):
                         column = gate_cols[:, r * T // P + b : r * T // P + b + 1]
                         nc.tensor.transpose(spread[:, b, :], column.to_broadcast([P, P]), identity[:])
-                    nc.vector.tensor_copy(out=gates[r][:], in_=spread[:].rearrange("p b c -> p (b c)"))
+                    nc.scalar.copy(out=gates[r][:], in_=spread[:].rearrange("p b c -> p (b c)"))
             if n == LAST_W2_AT:
                 last_rounded = round_w2(nc.vector.tensor_copy, w2_tile(N), load_w2(last, 0, N, RING, 0), 0)
 
@@ -241,13 +243,13 @@ def tile_moe_pkd_mlp_gelu_kernel(tc, x_words, x_scales, w1, w2, gate, offs, pos1
             if n - 1 in GELU_AFTER:
                 quantize_h(GELU_AFTER[n - 1], 0, C, h)
             if n in GELU_AFTER:
-                h = on_place(filled[-1], [P, C, PACK], BF16, "h%d" % n, 0)
+                h = on_place(place_of(min(n, 14)), [P, C, PACK], BF16, "h%d" % n, 0)
                 for half in range(2):
                     gelu(h[:, half * HALF : (half + 1) * HALF, :], pairs[GELU_AFTER[n]][half])
             if n == LAST_W2_AT:
                 last_q = quantize_w2(last_rounded)
             if o == 0:
-                pairs.append([banks.tile([P, PACK, HALF], F32, name="bank") for half in range(2)])
+                pairs.append([sums.tile([P, PACK, HALF], F32, name="bank") for half in range(2)])
             layer1_pass(pairs[e], n, words, scales)
 
         late = [(e, nt) for nt in range(N_TILES) for e in (2, 1, 0)]
@@ -282,9 +284,9 @@ def tile_moe_pkd_mlp_gelu_kernel(tc, x_words, x_scales, w1, w2, gate, offs, pos1
         make_y(banks, 0, [(q0a, 0, 0, 0, C), (q1a, 0, 1, 0, C)])
         make_y(banks, 0, [(q2a, 0, 2, 0, C), (last_q, 0, last, 0, HALF)])
         make_y(banks, 0, [(last_q, 0, last, HALF, C)])
-        make_y(banks, 1, [(q2b, 0, 2, 0, C), (last_q, P, last, 0, C)])
-        make_y(banks, 1, [(q1b, 0, 1, 0, C)])
-        make_y(banks, 1, [(q0b, 0, 0, 0, C)])
+        make_y(sums, 1, [(q2b, 0, 2, 0, C), (last_q, P, last, 0, C)])
+        make_y(sums, 1, [(q1b, 0, 1, 0, C)])
+        make_y(sums, 1, [(q0b, 0, 0, 0, C)])
 
         def fetch(nt, r, t0, t1):
             prod = stage.tile([P, t1 - t0], F32, name="prod%d_%d_%d" % (nt, r, t0), bufs=1)
@@ -330,7 +332,7 @@ def tile_moe_pkd_mlp_gelu_kernel(tc, x_words, x_scales, w1, w2, gate, offs, pos1
         turned = [stage.tile([P, mid], F32, name="turned", bufs=3) for part in range(3)]
         nc.scalar.copy(out=turned[2][:], in_=total[:].rearrange("p b n -> p (b n)"))
         for r in range(2):
-            bank = banks.tile([P, 2, P], F32, name="bank")
+            bank = sums.tile([P, 2, P], F32, name="bank")
             turn_blocks(bank, picked[r][:], True, True)
             for b in range(2):
                 column = gate_cols[:, r * T // P + b : r * T // P + b + 1]

from contextlib import ExitStack

import concourse.mybir as mybir
from concourse.masks import make_identity

K, T, E, C, H, N = 2560, 512, 4, 256, 512, 256
FLOPS = 2 * E * C * (K * H + H * N)

F32 = mybir.dt.float32
BF16 = mybir.dt.bfloat16
I32 = mybir.dt.int32
U32 = mybir.dt.uint32
U16 = mybir.dt.uint16
U8 = mybir.dt.uint8
FP8X4 = mybir.dt.float8_e4m3fn_x4
GELU = mybir.ActivationFunctionType.Gelu_apprx_tanh
COPY = mybir.ActivationFunctionType.Copy
MULT = mybir.AluOpType.mult
ADD = mybir.AluOpType.add

P = 128
PACK = 4
K_PASS = P * PACK
PASSES = K // K_PASS
CHUNKS = E * PASSES
QUADRANTS = 4
PLANES = 4
SLOTS = E * C
HALF = C // 2
PAIR = 2 * C
WINDOW = T + T // 2
N_TILES = N // P
LIST_ROWS = 16

RING = 10
PLACE_BYTES = 4 * PACK * H

SCALAR_ALONE = 7
VECTOR_ALONE = (7, 10, 14, 15)
SCALAR_TOO = (8, 11, 12)
T_HALF = PACK // 2
T_ORDER = (2, 3, 0, 1)
GELU_AFTER = {9: 0, 13: 1, 15: 2}
LAST_W2_AT = 12
LAST_SCALES_AT = 2
GATE_ROWS_AT = 8
LISTS_AFTER = 5
GATE_SPREAD_AT = 14


def tile_moe_pkd_mlp_gelu_kernel(tc, x_words, x_scales, w1, w2, gate, offs, pos1, pos2, out):
    nc = tc.nc
    with ExitStack() as ctx:
        keep = ctx.enter_context(tc.tile_pool(name="keep", bufs=1))
        ring = ctx.enter_context(tc.tile_pool(name="ring", bufs=1))
        stage = ctx.enter_context(tc.tile_pool(name="stage", bufs=4))
        codes = ctx.enter_context(tc.tile_pool(name="codes", bufs=2 * PASSES))
        turn = ctx.enter_context(tc.tile_pool(name="turn", bufs=1))
        sums = ctx.enter_context(tc.psum_pool(name="sums", bufs=4))
        banks = ctx.enter_context(tc.psum_pool(name="banks", bufs=3))
        turn_bank = ctx.enter_context(tc.psum_pool(name="turn_bank", bufs=1))

        offs_sb = keep.tile([P, SLOTS // LIST_ROWS], U16, name="offs_sb")
        pos_sb = [keep.tile([P, T // LIST_ROWS], U16, name="pos_sb%d" % r) for r in range(2)]
        tok_words = [keep.tile([P, WINDOW], I32, name="tok_words%d" % o, align_bytes=64) for o in range(PASSES)]
        tok_scales = [keep.tile([P, WINDOW], U8, name="tok_scales%d" % b, align_bytes=64) for b in range(2)]
        slot_words = [keep.tile([P, PASSES, PAIR], U32, name="slot_words%d" % g, align_bytes=64) for g in range(2)]
        slot_scales = [keep.tile([P, 2, PAIR], U8, name="slot_scales%d" % g, align_bytes=64) for g in range(2)]
        h_codes = [keep.tile([P, C], U32, name="h_codes%d" % e, align_bytes=64) for e in range(E)]
        h_scales = [keep.tile([P, C], U8, name="h_scales%d" % e, align_bytes=64) for e in range(E)]
        y_sb = [keep.tile([P, SLOTS], F32, name="y_sb%d" % nt) for nt in range(N_TILES)]

        filled = []

        def on_place(place, shape, dtype, name, skip):
            return ring.tile(shape, dtype, name=name, align_bytes=64, offset=place * PLACE_BYTES + skip)

        def load(shape, src, place, skip=0):
            filled.append(place)
            raw = on_place(place, shape, F32, "raw%d" % len(filled), skip)
            nc.sync.dma_start(out=raw[:], in_=src)
            return raw

        def place_of(n):
            return n if n < RING else (n - RING) ^ 1

        def w1_rows(n):
            e, o = divmod(n, PASSES)
            return w1[e, o * K_PASS : (o + 1) * K_PASS, :].rearrange("(p j) i -> p j i", j=PACK)

        def load_w2(e, n0, n1, place, skip):
            return load([P, PACK, n1 - n0], w2[e, :, n0:n1].rearrange("(p j) n -> p j n", j=PACK), place, skip)

        def load_scale_rows(b):
            o0, o1 = b * PLANES, min((b + 1) * PLANES, PASSES)
            for q in range(QUADRANTS):
                nc.sync.dma_start(
                    out=tok_scales[b][32 * q : 32 * q + 4 * (o1 - o0), 0:T].bitcast(I32),
                    in_=x_scales[o0:o1, 4 * q : 4 * q + 4, :].bitcast(I32),
                )

        def pair_list(g):
            return offs_sb[:, g * (PAIR // LIST_ROWS) : (g + 1) * (PAIR // LIST_ROWS)]

        def gather_tokens(o):
            for g in range(2):
                nc.vector.tensor_copy(out=slot_words[g][:, o, :], in_=tok_words[o][:].bitcast(U32).indirect(pair_list(g)))
                if o % PLANES == 0:
                    b = o // PLANES
                    nc.vector.tensor_copy(out=slot_scales[g][:, b, :], in_=tok_scales[b][:].indirect(pair_list(g)))

        def round_w1(grouped, raw, copies):
            dst = grouped.rearrange("p t m j -> p m j t")
            src = raw[:].rearrange("p j (m t) -> p m j t", t=PACK)
            share = PACK // len(copies)
            for i, copy in enumerate(copies):
                copy(out=dst[:, :, :, i * share : (i + 1) * share], in_=src[:, :, :, i * share : (i + 1) * share])

        def rounders(n):
            if n < SCALAR_ALONE or n in SCALAR_TOO:
                return [nc.scalar.copy]
            if n in VECTOR_ALONE:
                return [nc.vector.tensor_copy]
            return [nc.scalar.copy, nc.vector.tensor_copy]

        def quantize(words, scales, c0, c1, values):
            nc.vector.quantize_mx(out=words[:, c0:c1].bitcast(FP8X4), scales=scales[:, c0:c1], in_=values)

        def layer1_pass(pair, n, words, scales):
            e, o = divmod(n, PASSES)
            g = e // 2
            for half in range(2):
                slots = slice((e % 2) * C + half * HALF, (e % 2) * C + (half + 1) * HALF)
                for t in T_ORDER:
                    nc.tensor.matmul_mx(
                        out=pair[half][:, t, :],
                        lhsT=words[:, t * P : (t + 1) * P].bitcast(FP8X4),
                        lhsT_scale=scales[:, t * P : (t + 1) * P],
                        rhs=slot_words[g][:, o, slots].bitcast(FP8X4),
                        rhs_scale=slot_scales[g][4 * (o % PLANES) : P, o // PLANES, slots],
                        start=(o == 0 and t == T_ORDER[0]),
                        stop=(o == PASSES - 1 and t == T_ORDER[-1]),
                    )

        def gelu(dst, bank):
            nc.scalar.activation(out=dst, in_=bank[:].rearrange("p t s -> p s t"), func=GELU)

        def quantize_h(e, s0, s1, h):
            quantize(h_codes[e], h_scales[e], s0, s1, h[:].rearrange("p s t -> p (s t)"))

        def round_w2(copy, grouped, raw, n0):
            n1 = n0 + grouped.shape[1]
            copy(
                out=grouped[:].rearrange("p (c u) j -> p c j u", u=4),
                in_=raw[:, :, n0:n1].rearrange("p j (c u) -> p c j u", u=4),
            )
            return grouped

        def w2_tile(width):
            return stage.tile([P, width, PACK], BF16, name="w2_grouped", align_bytes=64, bufs=1)

        def quantize_w2(grouped):
            width = grouped.shape[1]
            words = stage.tile([P, width], U32, name="w2_codes", align_bytes=64, bufs=7)
            scales = stage.tile([P, width], U8, name="w2_scales", align_bytes=64, bufs=7)
            quantize(words, scales, 0, width, grouped[:].rearrange("p n j -> p (n j)"))
            return words, scales

        def make_y(pool, nt, parts):
            first_slot = parts[0][2] * C + parts[0][3]
            width = sum(s1 - s0 for w2q, n0, e, s0, s1 in parts)
            bank = pool.tile([P, width], F32, name="bank")
            for w2q, n0, e, s0, s1 in parts:
                c0 = e * C + s0 - first_slot
                nc.tensor.matmul_mx(
                    out=bank[:, c0 : c0 + s1 - s0],
                    lhsT=w2q[0][:, n0 : n0 + P].bitcast(FP8X4),
                    lhsT_scale=w2q[1][:, n0 : n0 + P],
                    rhs=h_codes[e][:, s0:s1].bitcast(FP8X4),
                    rhs_scale=h_scales[e][:, s0:s1],
                    start=True,
                    stop=True,
                )
            nc.scalar.copy(out=y_sb[nt][:, first_slot : first_slot + width], in_=bank[:])

        for b in range(2):
            nc.vector.memset(tok_scales[b][:].bitcast(I32), 0)
        for o in range(PASSES):
            nc.vector.memset(tok_words[o][:, T:], 0)
        identity = keep.tile([P, P], F32, name="identity")
        make_identity(nc, identity[:])
        gate_rows = keep.tile([P, P], F32, name="gate_rows")
        nc.gpsimd.memset(gate_rows[:], 0.0)
        gate_cols = keep.tile([P, 2 * T // P], F32, name="gate_cols")
        gates = [keep.tile([P, T], F32, name="gate_sb%d" % r) for r in range(2)]
        nc.sync.dma_start(offs_sb[:], offs)

        last = E - 1
        pairs = []
        for n in range(CHUNKS):
            e, o = divmod(n, PASSES)
            if e == 0:
                nc.sync.dma_start(out=tok_words[o][:, 0:T], in_=x_words[o].rearrange("p t r -> p (t r)").bitcast(I32))
            if n == 0:
                raw = load([P, PACK, H], w1_rows(n), place_of(n))
                load_scale_rows(0)
            if n == LAST_SCALES_AT:
                load_scale_rows(1)
            if e == 0:
                gather_tokens(o)
            if n == GATE_ROWS_AT:
                nc.sync.dma_start(out=gate_rows[0 : 2 * T // P, :], in_=gate[:, 0, :].rearrange("r (b c) -> r b c", c=P))
                gate_bank = turn_bank.tile([P, P], F32, name="bank")
                nc.tensor.transpose(gate_bank[:], gate_rows[:], identity[:])
                nc.vector.tensor_copy(out=gate_cols[:], in_=gate_bank[:, 0 : 2 * T // P])
            if n == GATE_SPREAD_AT:
                for r in range(2):
                    spread = sums.tile([P, T // P, P], F32, name="bank")
                    for b in range(T // P):
                        column = gate_cols[:, r * T // P + b : r * T // P + b + 1]
                        nc.tensor.transpose(spread[:, b, :], column.to_broadcast([P, P]), identity[:])
                    nc.scalar.copy(out=gates[r][:], in_=spread[:].rearrange("p b c -> p (b c)"))
            if n == LAST_W2_AT:
                last_rounded = round_w2(nc.vector.tensor_copy, w2_tile(N), load_w2(last, 0, N, RING, 0), 0)

            words = codes.tile([P, H], U32, name="w1_codes", align_bytes=64)
            scales = codes.tile([P, H], U8, name="w1_scales", align_bytes=64)
            if n < CHUNKS - 1:
                if n > 0:
                    raw = load([P, PACK, H], w1_rows(n), place_of(n))
                grouped = stage.tile([P, PACK, P, PACK], BF16, name="w1_grouped", align_bytes=64, bufs=8)
                round_w1(grouped[:], raw, rounders(n))
                quantize(words, scales, 0, H, grouped[:].rearrange("p t m j -> p (t m j)"))
            else:
                grouped = turn.tile([P, PACK, P, PACK], BF16, name="w1_last", tag="after_w1", align_bytes=64)
                for m0 in (0, P // 2):
                    raw = load([P, PACK, H // 2], w1_rows(n)[:, :, PACK * m0 : PACK * m0 + H // 2], place_of(n), m0 * 64)
                    round_w1(grouped[:, :, m0 : m0 + P // 2], raw, rounders(n))
                    for t in T_ORDER:
                        values = grouped[:, t, m0 : m0 + P // 2].rearrange("p m j -> p (m j)")
                        quantize(words, scales, t * P + m0, t * P + m0 + P // 2, values)

            if n - 1 in GELU_AFTER:
                quantize_h(GELU_AFTER[n - 1], 0, C, h)
            if n in GELU_AFTER:
                h = on_place(place_of(min(n, 14)), [P, C, PACK], BF16, "h%d" % n, 0)
                for half in range(2):
                    gelu(h[:, half * HALF : (half + 1) * HALF, :], pairs[GELU_AFTER[n]][half])
            if n == LAST_W2_AT:
                last_q = quantize_w2(last_rounded)
            if o == 0:
                pairs.append([sums.tile([P, PACK, HALF], F32, name="bank") for half in range(2)])
            layer1_pass(pairs[e], n, words, scales)

        late = [(e, nt) for nt in range(N_TILES) for e in (2, 1, 0)]
        raws = {}
        for i, (e, nt) in enumerate(late):
            raws[e, nt] = load_w2(e, nt * P, (nt + 1) * P, place_of(11 - i // 4), i % 4 * 2048)
            if i == LISTS_AFTER:
                nc.sync.dma_start(pos_sb[0][:], pos1)
                nc.sync.dma_start(pos_sb[1][:], pos2)

        def round_late(copy, e, nt):
            grouped = stage.tile([P, P, PACK], BF16, name="w2_late%d_%d" % (e, nt), align_bytes=64, bufs=1)
            return round_w2(copy, grouped, raws[e, nt], 0)

        rounded2a = round_late(nc.vector.tensor_copy, 2, 0)
        rounded1a = round_late(nc.scalar.copy, 1, 0)
        h_halves = [stage.tile([P, HALF, PACK], BF16, name="h_last%d" % half, align_bytes=64, bufs=1) for half in range(2)]
        for half in range(2):
            gelu(h_halves[half][:], pairs[last][half])
        q2a = quantize_w2(rounded2a)
        rounded0a = round_late(nc.vector.tensor_copy, 0, 0)
        q1a = quantize_w2(rounded1a)
        rounded2b = round_late(nc.vector.tensor_copy, 2, 1)
        quantize_h(last, 0, HALF, h_halves[0])
        q0a = quantize_w2(rounded0a)
        rounded1b = round_late(nc.vector.tensor_copy, 1, 1)
        quantize_h(last, HALF, C, h_halves[1])
        q2b = quantize_w2(rounded2b)
        rounded0b = round_late(nc.vector.tensor_copy, 0, 1)
        q1b = quantize_w2(rounded1b)
        q0b = quantize_w2(rounded0b)
        make_y(banks, 0, [(q0a, 0, 0, 0, C), (q1a, 0, 1, 0, C)])
        make_y(banks, 0, [(q2a, 0, 2, 0, C), (last_q, 0, last, 0, HALF)])
        make_y(banks, 0, [(last_q, 0, last, HALF, C)])
        make_y(sums, 1, [(q2b, 0, 2, 0, C), (last_q, P, last, 0, C)])
        make_y(sums, 1, [(q1b, 0, 1, 0, C)])
        make_y(sums, 1, [(q0b, 0, 0, 0, C)])

        def fetch(nt, r, t0, t1):
            prod = stage.tile([P, t1 - t0], F32, name="prod%d_%d_%d" % (nt, r, t0), bufs=1)
            entries = pos_sb[r][:, t0 // LIST_ROWS : t1 // LIST_ROWS]
            nc.vector.tensor_tensor(prod[:], y_sb[nt][:].indirect(entries), gates[r][:, t0:t1], MULT)
            return prod

        def finish(nt, t0, t1, first, second):
            res = stage.tile([P, t1 - t0], F32, name="res", bufs=4)
            nc.vector.tensor_tensor(res[:], first, second, ADD)
            nc.sync.dma_start(out=out[nt * P : (nt + 1) * P, t0:t1], in_=res[:])

        def turn_blocks(bank, src, start, stop):
            for b in range(2):
                nc.tensor.matmul(
                    out=bank[:, b, :],
                    lhsT=src[:, b * P : (b + 1) * P],
                    rhs=identity[:],
                    is_transpose=True,
                    start=start and b == 0,
                    stop=stop and b == 1,
                )

        def turn_back(nt, t0, parts):
            back = banks.tile([P, 2, P], F32, name="bank")
            for i, part in enumerate(parts):
                turn_blocks(back, part[:], i == 0, i == len(parts) - 1)
            res = stage.tile([P, 2 * P], F32, name="res", bufs=4)
            nc.scalar.copy(out=res[:], in_=back[:].rearrange("p b n -> p (b n)"))
            nc.scalar.dma_start(out=out[nt * P : (nt + 1) * P, t0 : t0 + 2 * P], in_=res[:])

        mid = T // 2
        products = [fetch(0, r, mid, T) for r in range(2)]
        first = fetch(1, 0, 0, T)
        seconds = [fetch(1, 1, t0, t0 + mid) for t0 in (0, mid)]

        picked = [stage.tile([P, mid], F32, name="picked%d" % r, bufs=1) for r in range(2)]
        for r in range(2):
            nc.scalar.activation(picked[r][:], y_sb[0][:].indirect(pos_sb[r][:, 0 : mid // LIST_ROWS]), COPY)
        total = banks.tile([P, 2, P], F32, name="bank")
        for r in range(2):
            turn_blocks(total, products[r][:], r == 0, r == 1)
        turned = [stage.tile([P, mid], F32, name="turned", bufs=3) for part in range(3)]
        nc.scalar.copy(out=turned[2][:], in_=total[:].rearrange("p b n -> p (b n)"))
        for r in range(2):
            bank = sums.tile([P, 2, P], F32, name="bank")
            turn_blocks(bank, picked[r][:], True, True)
            for b in range(2):
                column = gate_cols[:, r * T // P + b : r * T // P + b + 1]
                nc.scalar.activation(turned[r][:, b * P : (b + 1) * P], bank[:, b, :], COPY, scale=column)
        turn_back(0, mid, turned[2:])
        turn_back(0, 0, turned[:2])
        for t0, second in zip((0, mid), seconds):
            finish(1, t0, t0 + mid, first[:, t0 : t0 + mid], second[:])
